import numpy as np, ml_dtypes
CORES = [10,34,74,98]
N = 4
BF = ml_dtypes.bfloat16
M, L, S, E, G0, T, Q, W = 3520, 192, 64, 6, 3, 3, 1712, 3664
LV = [311, 518, 691, 829, 691, 416]
def forest(rng, lean):
    sn = np.full((16, M), M); fa = rng.integers(0, M, M); gn = np.zeros(M, np.int64)
    o = 64 + rng.permutation(M - 64); cur = np.arange(64); at = 0
    for i, n in enumerate(LV):
        nxt = o[at:at + n]; at += n
        share = 0.9 if i == 0 else 0.45 + 0.3 * rng.random()
        fert = rng.permutation(cur)[:max(n // 16 + 1, int(len(cur) * share))]
        key = rng.random((len(fert), 16)) * np.exp2(lean * rng.random((len(fert), 1)))
        pk = np.argsort(key.reshape(-1))[:n]; dad = fert[pk >> 4]
        sn[pk & 15, dad] = nxt; fa[nxt] = dad; gn[nxt] = i + 1; cur = nxt
    return sn, fa, gn
def woods(rng, lean):
    v = [forest(rng, lean) for _ in range(8 * N)]
    return np.stack([a[0] for a in v]).reshape(N, 8, 16, M), np.stack([a[1] for a in v]).reshape(N, 8, M), np.stack([a[2] for a in v]).reshape(N, 8, M)
def pack(x, w, sn, fa, gn):
    return {"x": np.ascontiguousarray(x.reshape(N, 128, M)).astype(np.float32).astype(BF), "w": np.ascontiguousarray(w.reshape(N, 128, 1)).astype(np.float32).astype(BF),
            "sn": np.ascontiguousarray(sn.reshape(N, 128, M)).astype(np.int32), "fa": fa.astype(np.int32), "gn": gn.astype(np.int32)}
def few(rng, sn, fa, gn, n):
    if n: sn[:, 64] = M; sn[:, M - 1] = M
    z = int(rng.integers(0, 64)); sn[:, z] = M
    empty = np.all(sn == M, axis=0); gn[empty] = np.minimum(gn[empty], G0 - 1)
    if n:
        o = np.flatnonzero(empty); o = rng.permutation(o[(o > 64) & (o < M - 1)])[:n - 2]
        o = np.concatenate([np.array([64, M - 1]), o]); fa[o] = z; gn[o] = G0 + rng.integers(0, 2, len(o))
def ladders(rng, sn, fa, gn):
    U = (E - 2) // 2 + 1; B = 2 * U + 4; nb = (M - 64) // B
    sn[:] = M; gn[:] = 0; fa[:] = rng.integers(0, 64, M)
    k = (64 + rng.permutation(M - 64))[:nb * B].reshape(nb, B); u = rng.integers(0, U + 1, nb); a = rng.integers(0, 16, nb)
    for j in range(U + 1):
        m = j <= u; up = k[m, j]; so = k[m, 1 + j]
        sn[a[m] if j == 0 else rng.integers(0, 16, len(up)), up] = so; fa[so] = up
    a = (a + 1 + rng.integers(0, 15, nb)) & 15
    for j in range(U + 2):
        m = j <= u + 1; up = k[m, 0 if j == 0 else U + 1 + j]; so = k[m, U + 2 + j]
        sn[a[m] if j == 0 else rng.integers(0, 16, len(up)), up] = so; fa[so] = up
    gn[k[np.arange(nb), 1 + u]] = G0 + rng.integers(0, 2, nb)
    sn[:4, :64] = rng.choice(k[:, 0], (4, 64))
def guests(rng, x, sn, fa, gn):
    n = S - int(rng.integers(0, 4)); z = int(rng.integers(1, 64)); o = 64 + rng.permutation(M - 64)
    last = M - 16 - np.arange(n); o = np.concatenate([last, o[~np.isin(o, last)]])
    s, p, q, y, h, r, u, v = o[:8 * n].reshape(8, n); h = np.sort(h)
    x[:] = rng.integers(0, 256, (16, M)); sn[:] = M; fa[:] = rng.integers(0, M, M); gn[:] = rng.integers(0, G0, M)
    deck = [np.arange(64)] + np.array_split(o[8 * n:], E)
    for a, b in zip(deck[:-1], deck[1:]):
        m = rng.random((16, len(a))) < 0.3; m[rng.integers(0, 16, len(a)), np.arange(len(a))] = True
        sn[:, a] = np.where(m, rng.choice(b, (16, len(a))), M); fa[b] = rng.choice(a, len(b))
    sn[:, z] = M
    for top, one, two in ((p, q, y), (y, h, r), (r, s, u)):
        i = rng.integers(0, 16, n); j = (i + rng.integers(1, 16, n)) & 15
        sn[i, top] = one; sn[j, top] = two; fa[one] = top; fa[two] = top
    sn[rng.integers(0, 16, n), s] = v; fa[v] = s; fa[h] = z; gn[q] = G0; gn[h] = G0
    x[:, h] = x[:, q]; x[:, r] = 255 - x[:, q]; x[:, u] = 255 - x[:, q]
    x[:, s] = x[:, q]; x[:8, s] = x[:8, s] ^ rng.integers(0, 2, (8, n))
def doubles(rng, o, x, sn, fa, gn, nought):
    n = len(o) // 8; p, g, y, z, v, u, a, b = o[:8 * n].reshape(8, n)
    h = 1 + rng.permutation(31)[:n]
    if nought: h[0] = 0
    sn[:, o] = M; sn[:, h] = M; fa[h] = p; fa[p] = g; gn[h] = G0
    up = np.arange(n) % 2 == 1; top = np.where(up, g, p); low = np.where(up, p, h); k = np.argsort(rng.random((n, 16)), axis=1).T
    sn[k[0], top] = low; sn[k[1], top] = low; sn[np.minimum(k[2], k[3]), top] = z; sn[np.maximum(k[2], k[3]), top] = y
    sn[k[4][up], p[up]] = h[up]; sn[k[5][up], p[up]] = h[up]
    sn[k[6], y] = v; sn[k[7], z] = u; sn[k[8], v] = a; sn[k[9], u] = b
    end = 255 * rng.integers(0, 2, (16, n)); m = rng.integers(0, 64, (16, n)) * ((np.arange(n) // 2) % 2)
    one = np.zeros((16, n), np.int64); one[rng.integers(0, 16, n), np.arange(n)] = 1
    x[:, h] = end; x[:, p] = end; x[:, z] = np.abs(255 - end - m); x[:, y] = np.abs(255 - end - m - one)
    return h
def setup_inputs(rng):
    sn, fa, gn = woods(rng, 3.0)
    return pack(rng.integers(0, 256, (N, 8, 16, M)), rng.integers(0, 16, (N, 8, 16, 1)), sn, fa, gn)
def setup_inputs_again(rng):
    sn, fa, gn = woods(rng, 2.0); base = rng.choice(np.array([0, 7, 130, 254]), (N, 8, 1, 1))
    x = base + np.where(rng.random((N, 8, 1, M)) < 0.75, rng.integers(0, 2, (N, 8, 1, M)), rng.integers(0, 2, (N, 8, 16, M)))
    for g in rng.permutation(8)[:4]:
        for q in range(N): guests(rng, x[q, g], sn[q, g], fa[q, g], gn[q, g])
    return pack(x, rng.integers(0, 16, (N, 8, 16, 1)), sn, fa, gn)
def setup_inputs_corners(rng):
    sn, fa, gn = woods(rng, 3.0)
    for q in range(N):
        for g, kind in enumerate(rng.permutation(8)):
            s, f_, n_ = sn[q, g], fa[q, g], gn[q, g]
            if kind < 6: few(rng, s, f_, n_, (S, S + 1, S - 1, L, L + 1, 0)[int(kind)])
            elif kind == 6:
                half = rng.permutation(M)[:M // 2]; s[:] = M; s[:, half] = rng.integers(0, M, (16, len(half)))
                f_[:] = rng.choice(half, M); n_[:] = rng.integers(0, E + 1, M)
            else: ladders(rng, s, f_, n_)
    return pack(rng.integers(0, 256, (N, 8, 16, M)), rng.integers(0, 16, (N, 8, 16, 1)), sn, fa, gn)
def setup_inputs_ends(rng):
    w = 15 * rng.integers(0, 2, (N, 8, 16, 1))
    for q in range(N):
        full, none = rng.permutation(8)[:2]
        if q == N - 1: full, none = 7, 0
        w[q, full] = 15; w[q, none] = 0
    x = 255 * np.where(rng.random((N, 8, 1, M)) < 0.6, rng.integers(0, 2, (N, 8, 1, M)), rng.integers(0, 2, (N, 8, 16, M))); x[..., 0] = 0; x[..., M - 1] = 255
    gn = E * rng.integers(0, 2, (N, 8, M)); sn = np.full((N, 8, 16, M), M)
    fa = np.where(rng.random((N, 8, M)) < 0.68, (M - 1) * rng.integers(0, 2, (N, 8, M)), rng.integers(0, M, (N, 8, M)))
    for q in range(N):
        for g in range(8):
            fer = rng.random(M) < 0.45; fer[:64] = True; fer[M - 1] = g % 2 == 0; fc = np.flatnonzero(fer)
            u = rng.random(M); m = rng.random((16, M)) < 0.3; m[:, u < 0.25] = False; m[15, u < 0.25] = True; m[:, u > 0.9] = True
            v = np.where(rng.random((16, M)) < 0.75, rng.choice(fc, (16, M)), rng.integers(0, M, (16, M)))
            v = np.where(rng.random((16, M)) < 0.12, (M - 1) * rng.integers(0, 2, (16, M)), v)
            sn[q, g] = np.where(m & fer, v, M); sn[q, g, 15, 0] = 0
            if g % 2 == 0:
                far = fc[np.all(x[q, g][:, fc] == 255, axis=0)]; sn[q, g, :, M - 1] = rng.choice(far, 16)
            else: gn[q, g, M - 1] = E; fa[q, g, M - 1] = rng.choice(fc)
    return pack(x, w, sn, fa, gn)
def setup_inputs_loops(rng):
    fa = rng.integers(0, M, (N, 8, M)); fa = np.where(rng.random((N, 8, M)) < 0.05, np.arange(M), fa)
    gn = rng.integers(0, E + 1, (N, 8, M)); sn = np.full((N, 8, 16, M), M); x = rng.integers(0, 256, (N, 8, 16, M))
    for q in range(N):
        for g in range(8):
            m = rng.random((16, M)) < rng.choice(np.array([0.0, 0.0, 0.06, 0.4, 1.0]), M)
            v = rng.integers(0, M, (16, M))
            if g % 2: v = rng.choice(rng.permutation(M)[:200], (16, M))
            v = np.where(rng.random((16, M)) < 0.03, np.arange(M), v); s = np.where(m, v, M)
            far = 64 + rng.permutation(M - 64); o = far[:192]; a, b, h = o[:64], o[64:128], o[128:]
            s[:, o] = M; s[5, a] = b; s[9, b] = h; s[11, b[:20]] = h[:20]; fa[q, g, h] = a; gn[q, g, h] = G0
            e = doubles(rng, far[192:384], x[q, g], s, fa[q, g], gn[q, g], g % 2 == 0)
            if g % 2:
                s[:, 32:64] = M; s[3, 32:64] = rng.choice(a, 32); s[:, 0] = M; fa[q, g, 0] = e[0]; gn[q, g, 0] = G0
            sn[q, g] = s
    return pack(x, rng.integers(0, 16, (N, 8, 16, 1)), sn, fa, gn)
def setup_inputs_spread(rng):
    sn, fa, gn = woods(rng, 9.0)
    x = (rng.random((N, 8, 16, M)) * np.exp2(8 * rng.random((N, 8, 1, M))) * (rng.random((N, 8, 1, M)) > 0.0625)).astype(np.int64)
    w = (rng.random((N, 8, 16, 1)) * np.exp2(4 * rng.random((N, 8, 16, 1)))).astype(np.int64)
    return pack(np.minimum(x, 255), np.minimum(w, 15), sn, fa, gn)
def check_inputs(d):
    bad = []
    for k, lo, hi in (("x", 0, 255), ("w", 0, 15), ("sn", 0, M), ("fa", 0, M - 1), ("gn", 0, E)):
        v = np.asarray(d[k]).astype(np.float64)
        if not (np.min(v) >= lo and np.max(v) <= hi): bad.append("range of " + k)
        elif np.any(v != np.floor(v)): bad.append("whole numbers in " + k)
    return bad
def narrow(tab, ix):
    return np.take_along_axis(tab, ix, 2)
def broad(tab, ix):
    return np.take_along_axis(tab, ix[:, :, None, :], 3)
def reference(x, w, sn, fa, gn):
    X = np.zeros((N, 8, 16, W), np.int32); X[..., :M] = x.astype(np.float32).reshape(N, 8, 16, M)
    SN = np.full((N, 8, 16, W), M, np.int64); SN[..., :M] = sn.reshape(N, 8, 16, M)
    F1 = np.zeros((N, 8, W), np.int64); F1[..., :M] = fa; F2 = F1.copy()
    GN = np.zeros((N, 8, W), np.int64); GN[..., :M] = gn
    wt = w.astype(np.float32).astype(np.int32).reshape(N, 8, 16, 1)
    ship_x = np.zeros((N, 8, 16, S), np.int32); ship_d = np.zeros((N, 8, S), np.int64); ship_h = np.full((N, 8, S), M)
    own = np.arange(L + S) < L; lower = np.tri(L, k=-1).astype(bool)
    for t in range(T):
        f = (F1 if t % 2 == 0 else F2).copy()
        order = (np.arange(W) + t * Q) % W
        ok = (np.all(SN == M, axis=2) & (GN >= G0))[..., order]; place = np.add.accumulate(ok.astype(np.int64), axis=2) - ok
        i, j, k = np.nonzero(ok & (place < L)); h = np.full((N, 8, L), M); h[i, j, place[i, j, k]] = order[k]
        xh = broad(X, h); ax = np.roll(ship_x, t, axis=0)
        xl = np.concatenate([xh, ax], axis=3); real = h != M
        live = np.concatenate([real, np.roll(ship_h, t, axis=0) != M], axis=2)
        c = np.concatenate([narrow(f, h), np.add.reduce(wt * ax, axis=2).astype(np.int64) & 63], axis=2); p = c.copy()
        b = np.concatenate([h, np.full((N, 8, S), M)], axis=2); up_n = np.ones((N, 8, L + S), np.int64)
        d = np.concatenate([np.full((N, 8, L), 2), np.roll(ship_d, t, axis=0)], axis=2)
        y = np.full((N, 8, L + S), M); s = y.copy(); a = np.zeros((N, 8, L + S), np.int64); found = np.zeros((N, 8, L + S), bool)
        for e in range(E):
            sons = broad(SN, c)
            can = (sons != M) & (sons != b[:, :, None, :])
            xs = broad(X, np.ascontiguousarray(sons.transpose(0, 1, 3, 2)).reshape(N, 8, -1)).reshape(N, 8, 16, L + S, 16)
            score = np.add.reduce(np.abs(xs - xl[..., None]), axis=2)
            best = np.argmin(np.where(can.transpose(0, 1, 3, 2), score, 2 ** 20), axis=3)
            son = np.take_along_axis(sons, best[:, :, None, :], 2)[:, :, 0]; some = np.any(can, axis=2)
            down = live & some; fail = live & ~some & (~own | (p < 64)); up = live & ~some & ~fail
            y = np.where(down, c, y); s = np.where(down, son, s); a = np.where(down, best, a); d = np.where(down, d - 1, d)
            hit = down & (d == 0); found = found | hit; live = live & ~fail & ~hit
            fp = narrow(f, p); up_n = np.where(up, up_n + 1, up_n); d = np.where(up, up_n + 1, d)
            b = np.where(up, p, np.where(down, M, b)); c = np.where(up, fp, np.where(down, son, c)); p = np.where(up, fp, p)
        fo, yo, so, ao = found[..., :L], y[..., :L], s[..., :L], a[..., :L]
        same = (yo[..., :, None] == yo[..., None, :]) | (so[..., :, None] == so[..., None, :])
        go = fo & ~np.any(same & fo[..., None, :] & lower, axis=3)
        several = np.add.reduce((broad(SN, yo) != M).astype(np.int64), axis=2) > 1
        mixed = (broad(X, so) + xh) >> 1
        back_x = np.roll(broad(X, s[..., L:]), -t, axis=0); back = np.roll(found[..., L:], -t, axis=0)
        lost = real & ~fo; place = np.add.accumulate(lost.astype(np.int64), axis=2) - lost; age = narrow(GN, h)
        i, j, k = np.nonzero(go); hh, yy, ss, aa = h[i, j, k], yo[i, j, k], so[i, j, k], ao[i, j, k]; m = several[i, j, k]
        SN[i, j, 0, hh] = ss; F2[i, j, ss] = hh; X[i, j, :, ss] = mixed[i, j, :, k]
        SN[i[m], j[m], aa[m], yy[m]] = M; F1[i[m], j[m], ss[m]] = hh[m]
        i, j, k = np.nonzero(back); hh = ship_h[i, j, k]; nc = M + 16 + S * (t - 1) + k
        X[i, j, :, nc] = back_x[i, j, :, k]; F1[i, j, nc] = hh; F2[i, j, nc] = hh; GN[i, j, nc] = GN[i, j, hh] + 1; SN[i, j, t, hh] = nc
        i, j, k = np.nonzero(lost & (place < S)); pl = place[i, j, k]
        ship_x = np.zeros((N, 8, 16, S), np.int32); ship_d = np.zeros((N, 8, S), np.int64); ship_h = np.full((N, 8, S), M)
        ship_x[i, j, :, pl] = xh[i, j, :, k]; ship_d[i, j, pl] = age[i, j, k]; ship_h[i, j, pl] = h[i, j, k]
    return {"xo": X.reshape(N, 128, W).astype(np.float32).astype(BF), "fo": F1.astype(np.float32), "f2o": F2.astype(np.float32)}

@@ -1,0 +1,692 @@
+from concourse.mybir import dt, AluOpType as A, AxisListType, ActivationFunctionType as F
+
+M, W, WX, EMPTY, EXT = 3520, 3664, 3920, 3520, 3856
+NB = 229
+KS = [[2, 2, 2, 2, 2, 2], [4, 4, 4, 3, 3, 3]]
+
+_sb = {
+    "SI": (3520, "int32"), "SN": (WX, "float32"), "X": (WX, "bfloat16"), "F1": (WX, "float32"), "F2": (WX, "float32"),
+    "GNR": (W, "bfloat16"), "GLR": (M, "bfloat16"), "NE": (M, "bfloat16"), "IOTA": (WX, "float32"), "ADD": (WX, "bfloat16"),
+    "GC": (320, "int32"), "FC": (320, "int32"), "FI": (640, "int32"), "FB": (640, "bfloat16"), "GB": (320, "bfloat16"),
+    "WT": (1, "bfloat16"), "I1": (256, "int32"), "PI": (1, "int32"), "PQ": (4, "int32"), "IP": (256, "int32"), "L15": (256, "int32"),
+    "IM": (12, "int32"), "COL": (16, "float32"), "MASK": (256, "float32"), "RES": (256, "float32"), "RESB": (256, "float32"),
+    "SLOT": (256, "bfloat16"), "LOWM": (192, "float32"), "JREP": (192, "float32"), "JK": (12, "float32"), "JS": (12, "float32"),
+    "BJ": (12, "float32"), "ARO": (64, "uint16"), "ONES": (1408, "bfloat16"), "REP": (1408, "bfloat16"), "BO": (128, "bfloat16"),
+    "BT": (128, "bfloat16"), "BO8": (8, "bfloat16"), "TMP": (128, "bfloat16"), "TM": (128, "bfloat16"), "TMX": (128, "bfloat16"),
+    "TRI": (128, "bfloat16"), "TRI2": (128, "bfloat16"), "IDN": (128, "bfloat16"), "NEGI": (128, "bfloat16"), "BIGI": (128, "bfloat16"),
+    "I255": (128, "bfloat16"), "SHU": (128, "bfloat16"), "SHD": (128, "bfloat16"),
+    "QD0": (128, "float32"), "QO0": (128, "float32"), "QD1": (128, "float32"), "QO1": (128, "float32"),
+    "LQ": (2048, "bfloat16"), "LQQ": (2048, "bfloat16"), "LW": (2048, "bfloat16"), "ONEF": (256, "float32"), "NEWT": (64, "float32"),
+    "NOK": (240, "bfloat16"), "OKR": (240, "bfloat16"), "SB": (240, "float32"), "PL": (240, "float32"), "CM0": (240, "float32"),
+    "CM1": (240, "float32"), "SJ": (240, "float32"), "KA": (12, "float32"), "KO": (12, "uint16"), "OH": (192, "bfloat16"),
+    "HB": (12, "float32"), "HT": (12, "float32"), "HE": (12, "float32"), "H": (12, "float32"), "HU": (12, "uint16"), "HREP": (192, "float32"),
+    "HRU": (192, "uint16"), "XLR": (4096, "bfloat16"), "G1": (192, "float32"), "G2": (192, "float32"), "P0": (12, "float32"),
+    "P0P": (12, "float32"), "Q1": (12, "float32"), "Q2": (12, "float32"), "PX": (12, "float32"), "PU": (12, "uint16"), "CU": (16, "uint16"),
+    "SUA": (128, "uint16"), "SUB": (128, "uint16"), "DFA": (2048, "bfloat16"), "DFB": (2048, "bfloat16"), "XGA": (1024, "bfloat16"),
+    "XGB": (1024, "bfloat16"), "SIGA": (128, "float32"), "SIGB": (128, "float32"), "EXA": (128, "float32"), "EXB": (128, "float32"),
+    "BXA": (128, "float32"), "BXB": (128, "float32"), "EQA": (128, "bfloat16"), "EQB": (128, "bfloat16"), "PMA": (128, "float32"),
+    "PMB": (128, "float32"), "FEA": (128, "float32"), "FEB": (128, "float32"), "MXA": (128, "float32"), "MXB": (128, "float32"),
+    "SXA": (8, "int32"), "SXB": (8, "int32"), "HI": (112, "int32"), "LG": (240, "float32"), "LO": (12, "bfloat16"),
+    "SLU": (12, "uint16"), "SR0": (384, "float32"), "SR1": (384, "float32"), "NTHI": (128, "bfloat16"), "UP1": (16, "float32"), "UP2": (16, "float32"), "G4": (64, "float32"), "G5": (64, "float32"), "SENT": (8, "float32"), "S4U": (4, "uint16"),
+    "GE": (16, "float32"), "AL": (32, "float32"), "RU": (4, "uint16"), "LU": (96, "uint16"), "YREP": (192, "float32"), "SREP": (192, "float32"),
+    "EZY": (192, "float32"), "EZS": (192, "float32"), "YX": (192, "float32"), "SX": (192, "float32"), "YM": (192, "float32"), "SM": (192, "float32"),
+    "DGY": (192, "bfloat16"), "DGS": (192, "bfloat16"), "EBY": (1056, "bfloat16"), "EBS": (1056, "bfloat16"), "SY": (192, "float32"),
+    "NY": (192, "bfloat16"), "EA": (192, "bfloat16"), "FF": (192, "float32"), "DS": (192, "float32"), "NC": (192, "float32"),
+    "SHA": (128, "float32"), "SHB": (128, "float32"), "HV": (192, "float32"), "MI": (192, "int32"), "MJ": (192, "int32"), "CC": (64, "float32"), "RT": (16, "float32"), "RLU": (16, "uint16"),
+}
+_apart = ("GC", "FC", "WT", "REP", "LQ", "LQQ", "LW")
+AT, _used = {}, {}
+for _k, (_n, _d) in _sb.items():
+    if _n <= 1056 and _k not in _apart:
+        AT[_k] = ("all_" + _d, _used.get(_d, 0), _n)
+        _used[_d] = _used.get(_d, 0) + (_n + 15) // 16 * 16
+    else:
+        AT[_k] = (_k, 0, _n)
+SCRATCH = {k: ("sbuf", [128, n], d) for k, (n, d) in _sb.items() if AT[k][0] == k}
+for _d, _n in _used.items(): SCRATCH["all_" + _d] = ("sbuf", [128, _n], _d)
+for _n in ("D3A", "D3B"): SCRATCH[_n] = ("sbuf", [128, 8, 256], "bfloat16")
+for _n in ("SGA", "SGB"): SCRATCH[_n] = ("sbuf", [128, 4, 32], "float32")
+for _n in ("PY0", "PY1", "LX1", "LX2", "RS1", "RS2", "RL1", "RL2"): SCRATCH[_n] = ("sbuf", [128, 72], "bfloat16")
+for _n in ("KEYA", "KEYB", "SUB0", "SUB1", "M0", "M1"): SCRATCH[_n] = ("psum", [128, 512], "float32")
+for _n in ("PWA", "PWB"): SCRATCH[_n] = ("psum", [128, 16, 32], "float32")
+PSUM = {k for k, v in SCRATCH.items() if v[0] == "psum"}
+SEMAPHORES = (["e_v", "e_s", "e_t", "e_g"] + ["ld%d" % i for i in range(12)] + ["st%d" % i for i in range(8)] + ["cp0"]
+              + ["snd_out%d" % i for i in (0, 1)] + ["snd_in%d" % i for i in (0, 1)] + ["ret_out%d" % i for i in (1, 2)] + ["ret_in%d" % i for i in (1, 2)])
+
+
+def rank_program(g, core, T, topo):
+    rank = T.rank_of(core)
+    if rank is None:
+        return
+    N = len(T.cores)
+    queue = {"v": g.vector, "s": g.scalar, "t": g.tensor, "g": g, "y": g.sync}
+    know = {q: {} for q in queue}
+    count = {}
+    clocks = {}
+    log = {}
+
+    def need(q, acc, write, deps):
+        name, lo, hi = acc
+        ps = name in PSUM
+        for l, h, w, q2, tok in log.get(name, ()):
+            if not ps and (h <= lo or hi <= l):
+                continue
+            if q2 == q and (q == "t" or not (w or write)):
+                continue
+            if w or write or (ps and q2 != q):
+                deps.add(tok)
+
+    def book(q, acc, write, tok):
+        name, lo, hi = acc
+        if name in PSUM:
+            lo, hi = 0, 1 << 20
+        old = log.setdefault(name, [])
+        if write or name in PSUM:
+            old[:] = [e for e in old if not (e[0] >= lo and e[1] <= hi)]
+        old.append((lo, hi, write, q, tok))
+
+    def waits(q, deps):
+        for tok in sorted(deps, key=lambda t: -t[1]):
+            sem, val = tok
+            if know[q].get(sem, 0) >= val:
+                continue
+            queue[q].wait_ge(T.sem[sem], val)
+            know[q][sem] = val
+            for s2, v2 in clocks[tok].items():
+                if know[q].get(s2, 0) < v2:
+                    know[q][s2] = v2
+
+    def call(q, fn, out, ins, extra, kw, sem=None, step=1):
+        reads = [a for o in ins if isinstance(o, tuple) for a in o[1]]
+        writes = list(out[1][:1])
+        reads += out[1][1:]
+        k2 = {}
+        for k, v in kw.items():
+            if isinstance(v, tuple):
+                (writes if k == "accum_out" else reads).extend(v[1])
+                k2[k] = v[0]
+            else:
+                k2[k] = v
+        deps = set()
+        for a in reads: need(q, a, False, deps)
+        for a in writes: need(q, a, True, deps)
+        waits(q, deps)
+        ins_ = fn(out[0], *[o[0] if isinstance(o, tuple) else o for o in ins], *extra, **k2)
+        sem = sem or "e_" + q
+        count[sem] = count.get(sem, 0) + step
+        ins_.then_inc(T.sem[sem], step)
+        tok = (sem, count[sem])
+        clocks[tok] = dict(know[q])
+        for a in reads: book(q, a, False, tok)
+        for a in writes: book(q, a, True, tok)
+
+    def b(name, lo=0, hi=None, st=1, p=None):
+        name, off, n = AT[name] if name in AT else (name, 0, SCRATCH[name][1][1])
+        lo, hi = lo + off, (n if hi is None else hi) + off
+        ap = T[name][:, lo:hi:st] if p is None else T[name][0:p, lo:hi:st]
+        return (ap, [(name, lo, hi)])
+
+    def c1(name, j): return b(name, j, j + 1)
+
+    def d3(name, lo, hi, a=None, z=None):
+        n = SCRATCH[name][1][2]
+        ap = T[name][:, lo:hi, :] if a is None else T[name][:, lo:hi, a:z]
+        return (ap, [(name, lo * n, hi * n)])
+
+    def ind(win, off, lo=0, hi=None):
+        w = b(win, 0, WX if hi is None else hi)
+        return (w[0].indirect(off[0]), w[1] + off[1])
+
+    V = g.vector
+    def tt(out, x, y, op): call("v", V.tensor_tensor, out, [x, y], [op], {})
+    def ts(out, x, s1, op, s2=None, op2=None):
+        if op2 is None: call("v", V.tensor_scalar, out, [x, s1], [None, op], {})
+        else: call("v", V.tensor_scalar, out, [x, s1, s2], [op, op2], {})
+    def cp(out, x): call("v", V.tensor_copy, out, [x], [], {})
+    def fill(out, c): call("v", V.memset, out, [], [c], {})
+    def scan(out, x, y, init, o0, o1): call("v", V.tensor_tensor_scan, out, [x, y], [init, o0, o1], {})
+    def act(out, x, f, **kw): call("s", g.scalar.activation, out, [x], [f], kw)
+    def mm(out, l, r, start, stop): call("t", g.tensor.matmul, out, [l, r], [start, stop], {})
+    def gop(fn, out, ins, extra, **kw): call("g", fn, out, ins, extra, kw)
+    def dma(q, out, x, sem):
+        o = out if isinstance(out, tuple) else (out, [])
+        deps = set()
+        rd = x[1] if isinstance(x, tuple) else []
+        for a in rd: need(q, a, False, deps)
+        for a in o[1]: need(q, a, True, deps)
+        waits(q, deps)
+        count[sem] = count.get(sem, 0) + 16
+        queue[q].dma_start(o[0], x[0] if isinstance(x, tuple) else x).then_inc(T.sem[sem], 16)
+        tok = (sem, count[sem])
+        clocks[tok] = dict(know[q])
+        for a in rd: book("dma", a, False, tok)
+        for a in o[1]: book("dma", a, True, tok)
+
+    def remote(to, dst, src, rsem, lsem):
+        peer = T.cores[to]
+        deps = set()
+        need("g", (src, 0, 72), False, deps)
+        waits("g", deps)
+        rid, pid, _ = topo.addr(peer)
+        n = len(topo.engines(core, peer))
+        g.remote_dma(T[dst][:], T[src][:], T.sem[rsem], T.sem[lsem], pid, rid, topo.mask(core, peer))
+        count[lsem] = n
+        book("rem", (src, 0, 72), False, (lsem, n))
+        clocks[(lsem, n)] = {}
+
+    def arrive(frm, buf, sem):
+        n = len(topo.engines(T.cores[frm], core))
+        count[sem] = n
+        clocks[(sem, n)] = {}
+        book("rem", (buf, 0, 72), True, (sem, n))
+
+    dma("y", b("GC", p=88), T.gn[:], "ld0")
+    dma("y", b("FC", p=88), T.fa[:], "ld1")
+    dma("y", b("WT"), T.w[:], "ld8")
+    for k in range(4):
+        dma("y" if k % 2 else "s", b("SI", 880 * k, 880 * k + 880), T.sn[:, 880 * k:880 * k + 880], "ld%d" % (2 + k))
+    dma("y", b("X", 0, 1760), T.x[:, 0:1760], "ld6")
+    dma("s", b("X", 1760, M), T.x[:, 1760:M], "ld7")
+
+    fill(b("ONES"), 1.0)
+    ia, af = g.iota, g.affine_select
+    def num(out, n, c, step=0):
+        gop(ia, out, [], [[[step, n]], c, 0], allow_small_or_imprecise_dtypes=True)
+    gop(ia, b("PI"), [], [[[1, 1]], 0, 1])
+    gop(af, b("REP"), [b("ONES")], [[[-1, 11], [-11, 8], [0, 16]], A.is_equal, 0.0, 0, 1])
+    gop(af, b("BT"), [b("ONES", 0, 128)], [[[-16, 8], [0, 16]], A.is_ge, 0.0, 0, 1])
+    gop(af, b("BO"), [b("BT")], [[[16, 8], [0, 16]], A.is_ge, 0.0, 15, -1])
+    gop(af, b("IDN"), [b("ONES", 0, 128)], [[[-1, 128]], A.is_equal, 0.0, 0, 1])
+    gop(af, b("TMP"), [b("BO")], [[[-1, 128]], A.is_ge, 0.0, 0, 1])
+    gop(af, b("TRI"), [b("BO")], [[[1, 128]], A.is_ge, 0.0, -1, -1])
+    gop(af, b("SHU"), [b("ONES", 0, 128)], [[[1, 128]], A.is_equal, 0.0, -16, -1])
+    gop(af, b("SHD"), [b("ONES", 0, 128)], [[[1, 128]], A.is_equal, 0.0, 16, -1])
+    num(b("GNR", M, W), W - M, 0)
+    num(b("OKR", 220, 240), 20, 0)
+    num(b("NOK", 220, 240), 20, 1)
+    num(b("PL", NB, 240), 240 - NB, 5000)
+    num(b("JREP"), 192, -255, 1)
+    gop(ia, b("IM"), [], [[[16, 12]], W, 0])
+    gop(ia, b("I1", 0, 192), [], [[[1, 192]], 0, 0])
+    gop(ia, b("IP"), [], [[[1, 256]], 128, -1])
+    gop(ia, b("L15"), [], [[[0, 16], [1, 16]], 0, 0])
+    gop(ia, b("SLOT"), [], [[[0, 16], [1, 16]], 0, 0], allow_small_or_imprecise_dtypes=True)
+    num(b("SN", M, WX), WX - M, 3520)
+    num(b("X", M, WX), WX - M, 0)
+    num(b("X", M, M + 1), 1, 4096)
+    for f in ("F1", "F2"):
+        num(b(f, M, EXT), EXT - M, 0)
+        num(b(f, M, M + 1), 1, 3520)
+        num(b(f, EXT, WX), WX - EXT, 3520)
+    num(b("IOTA"), WX, 0, 1)
+    for k in "AB":
+        num(b("EX" + k), 128, 4096)
+        num(b("EQ" + k), 128, 0)
+    for k in "12":
+        num(b("UP" + k), 16, 3520)
+    for k in "01":
+        num(b("SR" + k, 0, 64), 64, 3520)
+    for n in ("PY0", "PY1", "RS1", "RS2"): num(b(n, 64, 72), 8, 0)
+    num(b("ADD"), WX, 0)
+
+    cp(b("GB", p=88), b("GC", p=88))
+    ts(b("FI", 0, 320, p=88), b("FC", p=88), 6, A.arith_shift_right)
+    ts(b("FI", 320, 640, p=88), b("FC", p=88), 63, A.bitwise_and)
+    ts(b("FB", 0, 320, p=88), b("FI", 0, 320, p=88), 64.0, A.mult)
+    cp(b("FB", 320, 640, p=88), b("FI", 320, 640, p=88))
+    banks = ["SUB0", "SUB1", "M0", "M1"]
+    for r in range(11):
+        k = banks[r % 4]
+        mm(b(k, 0, 320), b("REP", 128 * r, 128 * r + 128, p=88), b("GB", p=88), True, True)
+        act(b("GNR", 320 * r, 320 * r + 320), b(k, 0, 320), F.Copy)
+    for r in range(11):
+        k = banks[(r + 3) % 4]
+        rep = b("REP", 128 * r, 128 * r + 128, p=88)
+        mm(b(k, 0, 320), rep, b("FB", 0, 320, p=88), True, False)
+        mm(b(k, 0, 320), rep, b("FB", 320, 640, p=88), False, True)
+        act(b("F1", 320 * r, 320 * r + 320), b(k, 0, 320), F.Copy)
+    dma("y", b("F2", 0, M), b("F1", 0, M), "cp0")
+    ts(b("PQ", 0, 1), b("PI"), 15, A.bitwise_and)
+    ts(b("PQ", 1, 2), b("PI"), 16, A.bitwise_and)
+    QC, I4, E0, C0, N1c, E1c, H0, H1, Q16, W16, QP = [c1("COL", j) for j in range(11)]
+    cp(QC, b("PQ", 0, 1))
+    ts(I4, b("PQ", 0, 1), 4096.0, A.mult, 4096.0, A.add)
+    ts(E0, b("PQ", 0, 1), 0, A.is_equal)
+    ts(C0, E0, -3520.0, A.mult, 3520.0, A.add)
+    ts(N1c, b("PQ", 0, 1), 1, A.not_equal)
+    ts(E1c, b("PQ", 0, 1), 1, A.is_equal)
+    ts(H0, b("PQ", 1, 2), 0, A.is_equal)
+    ts(H1, b("PQ", 1, 2), 0, A.not_equal)
+    ts(Q16, b("PQ", 0, 1), 0.0625, A.mult)
+    ts(b("BO8"), b("BO", 0, 128, 16), 16.0, A.mult)
+    fill(b("LQ"), 0.0)
+    for q in range(16):
+        cp((T.LQ[:, q * 128 + q:q * 128 + 128:16], [("LQ", q * 128, q * 128 + 128)]), b("BO8"))
+    ts(b("GLR"), b("GNR", 0, M), 3, A.is_lt)
+
+    def lq(q, name="LQ"): return b(name, 128 * q, 128 * q + 128)
+    for q in range(16):
+        mm(b("M0", 0, 220), lq(q), b("GLR", q, M, 16), q == 0, False)
+    for k in range(4):
+        cp(b("SN", 880 * k, 880 * k + 880), b("SI", 880 * k, 880 * k + 880))
+        act(b("NE", 880 * k, 880 * k + 880), b("SN", 880 * k, 880 * k + 880), F.Sign, bias=3520.0, scale=-1.0)
+    for q in range(16):
+        mm(b("M0", 0, 220), lq(q), b("NE", q, M, 16), False, q == 15)
+    ts(b("TM"), b("TMP"), -1.0, A.mult)
+    ts(b("I255"), b("IDN"), -255.0, A.mult)
+    tt(b("TMX"), b("TM"), b("I255"), A.add)
+    fill(b("ONEF"), 1.0)
+    ts(b("JK"), b("IM"), QC, A.add)
+    ts(b("JS"), b("JK"), -3472.0, A.add)
+    ts(b("BJ"), b("JK"), -3663.5, A.add)
+    ts(b("LQQ"), b("LQ"), Q16, A.mult)
+    ts(b("IP"), b("IP"), 15, A.bitwise_and)
+    ts(b("MASK"), b("IP"), 0, A.is_equal)
+    ts(b("RES"), b("L15"), 0, A.not_equal)
+    def late_constants():
+        ts(b("RESB"), b("RES"), -1e7, A.mult, 1e7, A.add)
+        ts(b("NEGI"), b("IDN"), -1.0, A.mult)
+        ts(b("NTHI"), b("IDN"), -524288.0, A.mult)
+        ts(b("BIGI"), b("IDN"), 4194304.0, A.mult)
+        ts(b("QD0"), b("IDN"), H0, A.mult)
+        ts(b("QD1"), b("IDN"), H1, A.mult)
+        ts(b("QO0"), b("SHU"), H0, A.mult)
+        ts(b("QO1"), b("SHD"), H1, A.mult)
+
+    def later_constants():
+        ts(W16, b("WT"), 0.0625, A.mult)
+        ts(b("LW"), b("LQ"), W16, A.mult)
+        ts(QP, b("PQ", 0, 1), 1.0, A.add)
+        for k in "YS":
+            ts(b("EZ" + k), b("L15", 0, 192), QP, A.is_equal, -20000.0, A.mult)
+        cp(b("ARO"), b("I1", 0, 64))
+        ts(b("TRI2"), b("TRI"), 2.0, A.mult)
+        tt(b("TRI2"), b("TRI2"), b("IDN"), A.subtract)
+        ts(b("NEWT"), b("I1", 0, 64), 3536.0, A.add, E1c, A.mult)
+
+    def lg(j, n=12, lo=0): return b("LG", 12 * j + lo, 12 * j + lo + n)
+
+    def diag(out, x, n, g1="G1", g2="G2"):
+        tt(b(g1, 0, n), x, b("MASK", 0, n), A.mult)
+        scan(b(g2, 0, n), b("RES", 0, n), b(g1, 0, n), 0.0, A.mult, A.add)
+        cp(out, b(g2, 15, n, 16))
+
+    def recount():
+        mm(b("M0", 0, NB), b("IDN"), b("NOK", 0, NB), True, False)
+        for q in range(16):
+            mm(b("M0", 0, NB), lq(q), b("ADD", q, W, 16), False, q == 15)
+
+    def lanes(t, meanwhile):
+        r = 107 * t % NB
+        sign = 9 if t else 10
+        if t == 0:
+            ts(b("OKR", 0, 220), b("M0", 0, 220), 0, A.is_equal)
+            ts(b("NOK", 0, 220), b("M0", 0, 220), 0, A.not_equal)
+        else:
+            ts(b("OKR", 0, NB - r), b("M0", r, NB), 0, A.is_equal)
+            ts(b("OKR", NB - r, NB), b("M0", 0, r), 0, A.is_equal)
+        mm(b("M1", 0, NB), b("BO"), b("OKR", 0, NB), True, True)
+        mm(b("M1", 240, 240 + NB), b("TMX"), b("OKR", 0, NB), True, True)
+        scan(b("SB", 0, NB), b("ONEF", 0, NB), b("M1", 0, NB), 0.0, A.mult, A.add)
+        for m in range(sign):
+            act(b("SJ", 0, NB), b("SB", 0, NB), F.Sign, bias=c1("BJ", m), scale=-1.0, accum_out=c1("KA", m))
+        tt(b("PL", 0, NB), b("M1", 240, 240 + NB), b("SB", 0, NB), A.add)
+        for m in range(sign, 12):
+            ts(b("CM%d" % (m % 2), 0, NB), b("SB", 0, NB), c1("BJ", m), A.is_le)
+            call("v", V.tensor_reduce, c1("KA", m), [b("CM%d" % (m % 2), 0, NB)], [AxisListType.X, A.add], {})
+        meanwhile()
+        ts(b("KA", 0, sign), b("KA", 0, sign), 0.5, A.mult, NB / 2.0, A.add)
+        cp(b("KO"), b("KA"))
+        tt(b("OH"), ind("PL", b("KO"), hi=240), b("JREP"), A.is_equal)
+        for q in range(16):
+            mm(b("M0", 0, 12), lq(q, "LQQ"), b("OH", q, 192, 16), q == 0, q == 15)
+        ts(b("HT"), b("KA"), NB - r, A.is_ge, -float(NB), A.mult)
+        ts(b("HE"), b("KA"), NB, A.is_ge, 3520.0 - 16 * r, A.mult)
+        tt(b("HT"), b("HT"), b("KA"), A.add)
+        ts(b("HB"), b("HT"), 16.0, A.mult, 16.0 * r, A.add)
+        tt(b("HB"), b("HB"), b("HE"), A.add)
+        tt(b("H"), b("M0", 0, 12), b("HB"), A.add)
+        cp(b("HU"), b("H"))
+
+    def climb(F_, src, out):
+        ts(b("PX"), src, 64, A.is_lt, float(EXT), A.mult)
+        tt(b("PX"), b("PX"), src, A.add)
+        cp(b("PU"), b("PX"))
+        tt(b("G1"), ind(F_, b("PU")), b("MASK", 0, 192), A.mult)
+        scan(b("G2"), b("RES", 0, 192), b("G1"), 0.0, A.mult, A.add)
+        cp(out, b("G2", 15, 192, 16))
+
+    def starts(t):
+        F_ = "F2" if t % 2 else "F1"
+        cp(b("HRU"), ind("IOTA", b("HU")))
+        act(b("XLR", 1280, 2048), ind("X", b("HRU", 48, 96)), F.Copy)
+        tt(b("G1"), ind(F_, b("HU")), b("MASK", 0, 192), A.mult)
+        scan(b("G2"), b("RES", 0, 192), b("G1"), 0.0, A.mult, A.add)
+        cp(b("CU", 2, 14), b("G2", 15, 192, 16))
+        cp(b("P0"), b("G2", 15, 192, 16))
+        if t:
+            if t == 1: fill(b("EQA", 0, 32), 0.0)
+            LX = "LX%d" % t
+            for q in range(16):
+                mm(b("M1", 0, 4), lq(q, "LW"), b(LX, q, 64, 16), q == 0, q == 15)
+            act(b("XLR", 0, 512), ind(LX, b("ARO", 0, 32), hi=64), F.Copy)
+            cp(b("HI", 0, 4), b("M1", 0, 4))
+            ts(b("HI", 0, 4), b("HI", 0, 4), 63, A.bitwise_and)
+            ts(b("AL", 0, 4), b(LX, 64, 68), 3, A.is_lt)
+            ts(b("AL", 4, 8), b("HI", 0, 4), -1.0, A.mult, 3520.0, A.add)
+            tt(b("AL", 4, 8), b("AL", 4, 8), b("AL", 0, 4), A.mult)
+            tt(b("AL", 4, 8), b("AL", 4, 8), b("HI", 0, 4), A.add)
+            cp(b("CU", 0, 2), b("AL", 4, 6))
+            cp(b("CU", 14, 16), b("AL", 6, 8))
+
+    def starts_a(t):
+        cp(b("XLR", 512, 1280), ind("X", b("HRU", 0, 48)))
+
+    def starts_b(t):
+        act(b("XLR", 2048, 3584), ind("X", b("HRU", 96, 192)), F.Copy)
+        if t:
+            act(b("XLR", 3584, 4096), ind("LX%d" % t, b("ARO", 32, 64), hi=64), F.Copy)
+
+    def hist(e, lo, hi): return b("HI", 16 * e + lo, 16 * e + hi)
+
+    def rng(t, z):
+        if z == "A": return (0 if t else 2), 8, 2, 8
+        return 8, (16 if t else 14), 8, 14
+
+    Z1, Z2, REAL, DQ, DP, ALB, TA, TB, SA, YA, MA, FO, MB = range(13)
+    UP = {1: "UP1", 2: "UP2"}
+
+    def front(t, e, z, between=None, behind=None):
+        k0, k1, o0, o1 = rng(t, z)
+        kc = k1 - k0
+        n = 16 * kc
+        ks = KS[1 if t else 0][e - 1]
+        kv = kc - ks
+        cu = b("CU", k0, k1)
+        su, df, xg, sg, dd, pw, key = "SU" + z, "DF" + z, "XG" + z, "SG" + z, "D3" + z, "PW" + z, "KEY" + z
+        sub = ("SUB0", "M0") if z == "A" else ("SUB1", "M1")
+        nb = kc // 2
+        act(b("SH" + z, 0, n), ind("SN", cu), F.Identity, bias=I4)
+        cp(b(su, 0, n), ind("SN", cu))
+        act(d3(sg, 0, nb), b("SH" + z, 0, n), F.Copy)
+        if between: between()
+        for P in (0, 1):
+            mm(d3(pw, 0, nb, 16 * P, 16 * P + 16), b("QD%d" % P), d3(sg, 0, nb, 16 * P, 16 * P + 16), True, False)
+            mm(d3(pw, 0, nb, 16 * P, 16 * P + 16), b("QO%d" % P), d3(sg, 0, nb, 16 - 16 * P, 32 - 16 * P), False, True)
+        act(b(xg, 0, 256 * ks), ind("X", b(su, 16 * kv, n)), F.Copy)
+        if behind: behind()
+        x0 = 256 * k0
+        c4 = min(kv, 4)
+        tt(b(df, 0, 256 * c4), ind("X", b(su, 0, 16 * c4)), b("XLR", x0, x0 + 256 * c4), A.subtract)
+        if kv > 4:
+            tt(b(df, 1024, 256 * kv), ind("X", b(su, 64, 16 * kv)), b("XLR", x0 + 1024, x0 + 256 * kv), A.subtract)
+        subs = [(kv + 2 * j, min(kv + 2 * j + 2, kc), sub[j]) for j in range((ks + 1) // 2)]
+        for lo, hi, bank in subs:
+            w = 256 * (hi - lo)
+            mm(b(bank, 0, w), b("IDN"), b(xg, 256 * (lo - kv), 256 * (hi - kv)), True, False)
+            mm(b(bank, 0, w), b("NEGI"), b("XLR", x0 + 256 * lo, x0 + 256 * hi), False, True)
+        act(d3(dd, 0, c4), b(df, 0, 256 * c4), F.Abs)
+        for lo, hi, bank in subs:
+            act(d3(dd, lo, hi), b(bank, 0, 256 * (hi - lo)), F.Abs)
+        if kv > 4:
+            act(d3(dd, 4, kv), b(df, 1024, 256 * kv), F.Abs)
+        sig = b("SIG" + z, 0, n)
+        if e <= 3:
+            i0, i1 = o0 - k0, o1 - k0
+            m0, m1 = o0 - 2, o1 - 2
+            ex = b("EX" + z, 16 * i0, 16 * i1, 16)
+            L = m1 - m0
+            my, ta, tb = "MX" + z, lg(TA, L, m0), lg(TB, L, m0)
+            if e == 1:
+                ts(ex, b("H", m0, m1), 4096.0, A.add)
+            else:
+                Z = lg(Z1 if e == 2 else Z2, L, m0)
+                ts(Z, b(my, 16 * i0 + 15, 16 * i1, 16), 4096, A.is_lt)
+                tt(ta, Z, b("P0P", m0, m1) if e == 2 else lg(ALB, L, m0), A.mult)
+                if e == 2:
+                    tt(tb, Z, lg(DQ, L, m0), A.mult)
+                ts(ex, ta, 4095.0, A.add)
+                if e == 2:
+                    tt(b("UP2", o0, o1), tb, b("UP1", o0, o1), A.add)
+                    tt(ta, Z, lg(DP, L, m0), A.mult)
+                    tt(lg(ALB, L, m0), ta, b("P0P", m0, m1), A.add)
+            scan(b("BX" + z, 16 * i0, 16 * i1), b("RES", 0, 16 * L), b("EX" + z, 16 * i0, 16 * i1), 0.0, A.mult, A.add)
+        call("v", V.transpose, sig, [d3(pw, 0, nb)], [], {})
+        if e <= 3:
+            tt(b("EQ" + z, 16 * i0, 16 * i1), b("SIG" + z, 16 * i0, 16 * i1), b("BX" + z, 16 * i0, 16 * i1), A.is_equal)
+        for lo, hi in ((0, c4), (c4, kc)):
+            o = b(key, 16 * lo, 16 * hi)
+            mm(o, b("IDN"), b("SLOT", 16 * lo, 16 * hi), True, False)
+            if e <= 3:
+                mm(o, b("NTHI"), b("ONES", 16 * lo, 16 * hi), False, False)
+            for q in range(16):
+                mm(o, lq(q), d3(dd, lo, hi, 16 * q, 16 * q + 16), False, q == 15 and e > 3)
+            if e <= 3:
+                mm(o, b("BIGI"), b("EQ" + z, 16 * lo, 16 * hi), False, True)
+
+    def back(t, e, z):
+        k0, k1, o0, o1 = rng(t, z)
+        kc = k1 - k0
+        n = 16 * kc
+        key, pm, fe, mx, sx = b("KEY" + z, 0, n), b("PM" + z, 0, n), b("FE" + z, 0, n), b("MX" + z, 0, n), b("SX" + z, 0, kc)
+        if e <= 3: scan(pm, b("RES", 0, n), key, 0.0, A.mult, A.min)
+        else: scan(pm, b("RESB", 0, n), key, 1e7, A.add, A.min)
+        tt(fe, key, pm, A.is_equal)
+        tt(fe, fe, b("SIG" + z, 0, n), A.mult)
+        f0 = b("FE" + z, 0, n, 16)
+        if e <= 2: tt(f0, f0, b(UP[e], k0, k1), A.max)
+        elif e == 3: ts(f0, f0, 3520, A.max)
+        scan(mx, b("RES", 0, n), fe, 0.0, A.mult, A.max)
+        cp(sx, b("MX" + z, 15, n, 16))
+        ts(hist(e, k0, k1), sx, 4095, A.bitwise_and)
+        if e < 6:
+            cp(b("CU", k0, k1), hist(e, k0, k1))
+
+    def acc(dst, m, e, first=False):
+        tt(lg(TB), lg(m), hist(e, 2, 14), A.mult)
+        tt(lg(dst), lg(dst), lg(TB), A.add)
+
+    def arr(e):
+        LXg = b("GE", 4 * (e - 3), 4 * (e - 3) + 4)
+        tt(b("AL", 12, 14), b("GE", 4 * (e - 3), 4 * (e - 3) + 2), hist(e, 0, 2), A.mult)
+        tt(b("AL", 14, 16), b("GE", 4 * (e - 3) + 2, 4 * (e - 3) + 4), hist(e, 14, 16), A.mult)
+        if e == 3: ts(b("AL", 16, 20), b("AL", 0, 4), 3520.0, A.mult)
+        tt(b("AL", 16, 20), b("AL", 16, 20), b("AL", 12, 16), A.add)
+
+    def partial(t):
+        ts(lg(MA), lg(Z1), -1.0, A.mult, 1.0, A.add)
+        ts(lg(MB), lg(Z2), -1.0, A.mult, 1.0, A.add)
+        tt(lg(13), lg(MA), lg(MB), A.mult)
+        tt(lg(14), lg(Z1), lg(MB), A.mult)
+        tt(lg(15), lg(MA), lg(Z2), A.mult)
+        tt(lg(16), lg(Z1), lg(Z2), A.mult)
+        tt(lg(SA), lg(13), hist(2, 2, 14), A.mult)
+        tt(lg(YA), lg(13), hist(1, 2, 14), A.mult)
+        acc(SA, 14, 4)
+        acc(YA, 14, 3)
+        acc(SA, 15, 5)
+        acc(YA, 15, 4)
+        acc(YA, 16, 5)
+        if t:
+            for e in (3, 4, 5, 6):
+                ts(b("GE", 4 * (e - 3), 4 * (e - 3) + 4), b("LX%d" % t, 64, 68), e, A.is_equal)
+            for e in (3, 4, 5): arr(e)
+
+    def give_back(t):
+        rs = "RS%d" % t
+        arr(6)
+        ts(b("AL", 20, 24), b("AL", 16, 20), 3520, A.is_equal)
+        ts(b(rs, 64, 68), b("AL", 16, 20), 3520, A.not_equal)
+        tt(b("AL", 24, 28), b("AL", 16, 20), b("AL", 20, 24), A.add)
+        cp(b("RU"), b("AL", 24, 28))
+        cp(b(rs, 0, 64), ind("X", b("RU")))
+        remote((rank - t) % N, "RL%d" % t, rs, "ret_in%d" % t, "ret_out%d" % t)
+
+    def send(t):
+        py, SE = "PY%d" % t, b("SENT", 4 * t, 4 * t + 4)
+        tt(b("LO"), lg(REAL), lg(FO), A.subtract)
+        mm(b("M1", 0, 12), b("BO"), b("LO"), True, True)
+        mm(b("M1", 16, 28), b("TM"), b("LO"), True, True)
+        scan(lg(TA), b("ONEF", 0, 12), b("M1", 0, 12), 0.0, A.mult, A.add)
+        tt(lg(TA), b("M1", 16, 28), lg(TA), A.add)
+        tt(lg(TA), lg(TA), b("JS"), A.subtract)
+        tt(lg(TA), lg(TA), b("LO"), A.mult)
+        tt(lg(TA), lg(TA), b("JS"), A.add)
+        cp(b("SLU"), lg(TA))
+        sr = "SR%d" % t
+        w = ind(sr, b("SLU"), hi=384)
+        cp(w, b("HREP"))
+        diag(b("S4U"), b(sr, 0, 64), 64, "G4", "G5")
+        cp(SE, b("S4U"))
+        cp(b(py, 0, 64), ind("X", b("S4U")))
+        tt(b("G4"), ind("GNR", b("S4U"), hi=W), b("MASK", 0, 64), A.mult)
+        scan(b("G5"), b("RES", 0, 64), b("G4"), 0.0, A.mult, A.add)
+        cp(b(py, 64, 68), b("G5", 15, 64, 16))
+        remote((rank + 1 + t) % N, "LX%d" % (t + 1), py, "snd_in%d" % t, "snd_out%d" % t)
+
+    def choose(out, base, cond, val):
+        tt(lg(TA), val, base, A.subtract)
+        tt(lg(TA), lg(TA), cond, A.mult)
+        tt(out, lg(TA), base, A.add)
+
+    def adopt(t):
+        last = t == 2
+        YL, SL, GO, SV, LT = lg(13), lg(SA), lg(15), lg(16), lg(17)
+        cp(b("LU", 12, 24), SL)
+        act(b("SREP"), ind("IOTA", b("LU", 12, 24)), F.Copy)
+        ts(lg(TA), lg(YA), -3520.0, A.add)
+        tt(lg(TA), lg(TA), lg(FO), A.mult)
+        ts(YL, lg(TA), 3520.0, A.add)
+        cp(b("LU", 0, 12), YL)
+        act(b("YREP"), ind("IOTA", b("LU", 0, 12)), F.Copy)
+        tt(b("MI"), ind("X", b("LU", 12, 24)), b("XLR", 512, 3584, 16), A.add)
+        ts(b("EZY", 0, 192, 16), YL, 20000.0, A.add)
+        scan(b("YX"), b("RES", 0, 192), b("EZY"), 0.0, A.mult, A.add)
+        ts(b("EZS", 0, 192, 16), SL, 20000.0, A.add)
+        scan(b("SX"), b("RES", 0, 192), b("EZS"), 0.0, A.mult, A.add)
+        off = [0]
+        for k in range(11): off.append(off[-1] + 176 - 16 * k)
+        for nm, li, st in (("S", SA, True), ("Y", 13, False)):
+            rep = nm + "REP"
+            tt(b("DG" + nm), b(rep), b(nm + "X"), A.is_equal)
+            for k in range(11):
+                ts(b("EB" + nm, off[k], off[k + 1]), b(rep, 16 * k + 16, 192), b("LG", 12 * li + k, 12 * li + k + 1), A.is_equal)
+            mm(b("M1", 0, 192), b("BO"), b("DG" + nm), st, False)
+            for k in range(11):
+                mm(b("M1", 16 * k + 16, 192), b("BO"), b("EB" + nm, off[k], off[k + 1]), False, k == 10 and not st)
+        cp(b("SY"), ind("SN", b("LU", 0, 12)))
+        ts(b("NY"), b("SY"), 3520, A.not_equal)
+        for q in range(16):
+            mm(b("SUB1", 0, 12), lq(q), b("NY", q, 192, 16), q == 0, q == 15)
+        if not last:
+            tt(b("EA"), b("SY"), b("SREP"), A.is_equal)
+            mm(b("SUB0", 0, 192), b("TRI2"), b("EA"), True, True)
+            act(b("DS"), b("SREP"), F.Copy, bias=3520.0, scale=-1.0)
+        tt(b("G1"), b("M1", 0, 192), b("MASK", 0, 192), A.mult)
+        scan(b("G2"), b("RES", 0, 192), b("G1"), 0.0, A.mult, A.add)
+        ts(GO, b("G2", 15, 192, 16), 0, A.is_equal)
+        tt(GO, GO, lg(FO), A.mult)
+        if not last:
+            choose(LT, b("JK"), GO, b("H"))
+            cp(b("LU", 36, 48), LT)
+            cp(ind("ADD", b("LU", 36, 48)), b("ONES", 0, 192))
+
+    def write_men(t):
+        last = t == 2
+        YL, SL, GO, SV, LT = lg(13), lg(SA), lg(15), lg(16), lg(17)
+        ts(b("MJ"), b("MI"), 1, A.arith_shift_right)
+        choose(LT, b("JK"), GO, SL)
+        cp(b("LU", 24, 36), LT)
+        cp(ind("X", b("LU", 24, 36)), b("MJ"))
+        if last: dma("y", T.xo[:, 0:M], b("X", 0, M), "st0")
+        ts(SV, b("SUB1", 0, 12), 24, A.is_gt)
+        tt(SV, SV, GO, A.mult)
+        cp(ind("F2", b("LU", 24, 36)), b("HREP"))
+        choose(LT, b("JK"), SV, SL)
+        cp(b("LU", 60, 72), LT)
+        cp(ind("F1", b("LU", 60, 72)), b("HREP"))
+
+    def write_sons(t):
+        YL, SV, LT = lg(13), lg(16), lg(17)
+        ts(b("HV"), b("SREP"), E0, A.mult, C0, A.add)
+        cp(ind("SN", b("LU", 36, 48)), b("HV"))
+        ts(b("FF"), b("SUB0", 0, 192), -1, A.is_equal)
+        tt(b("FF"), b("FF"), b("DS"), A.mult)
+        tt(b("NC"), b("FF"), b("SY"), A.add)
+        choose(LT, b("JK"), SV, YL)
+        cp(b("LU", 48, 60), LT)
+        cp(ind("SN", b("LU", 48, 60)), b("NC"))
+        if t == 1:
+            ts(b("CC"), ind("SN", b("RLU", 4, 8)), N1c, A.mult)
+            tt(b("CC"), b("CC"), b("NEWT"), A.add)
+            cp(ind("SN", b("RLU", 4, 8)), b("CC"))
+
+    def get_back(t):
+        rl = "RL%d" % t
+        SE, fl = b("SENT", 4 * (t - 1), 4 * t), b(rl, 64, 68)
+        arrive((rank + t) % N, rl, "ret_in%d" % t)
+        if t == 1:
+            ts(b("NOK", 221, 225), fl, -1.0, A.mult, 1.0, A.add)
+            tt(b("RT", 4, 8), SE, b("JK", 0, 4), A.subtract)
+            tt(b("RT", 4, 8), b("RT", 4, 8), fl, A.mult)
+            tt(b("RT", 4, 8), b("RT", 4, 8), b("JK", 0, 4), A.add)
+            cp(b("RLU", 4, 8), b("RT", 4, 8))
+            cp(ind("ADD", b("RLU", 4, 8)), b("ONES", 0, 64))
+
+    def new_men(t):
+        rl, nc = "RL%d" % t, 3536 + 64 * (t - 1)
+        cp(b("X", nc, nc + 64), b(rl, 0, 64))
+        tt(b("RT", 0, 4), b("SENT", 4 * (t - 1), 4 * t), b(rl, 64, 68), A.mult)
+        cp(b("RLU", 0, 4), b("RT", 0, 4))
+        cp(b("F1", nc, nc + 64), ind("IOTA", b("RLU", 0, 4)))
+        cp(b("F2", nc, nc + 64), b("F1", nc, nc + 64))
+
+    def rest(t):
+        write_sons(t)
+        if t: new_men(t)
+
+    for t in range(3):
+        lanes(t, (lambda: rest(t - 1)) if t else late_constants)
+        ts(lg(REAL), b("H"), 3520, A.not_equal)
+        if t:
+            arrive((rank - t) % N, "LX%d" % t, "snd_in%d" % (t - 1))
+        starts(t)
+        F_ = "F2" if t % 2 else "F1"
+        q1, q2 = b("UP1", 2, 14), b("Q2")
+        front(t, 1, "A", lambda: starts_a(t), lambda: starts_b(t))
+        front(t, 1, "B", None if t else later_constants)
+        act(b("HREP"), ind("IOTA", b("HU")), F.Copy)
+        climb(F_, b("P0"), q1)
+        climb(F_, q1, q2)
+        ts(b("P0P"), b("P0"), 1.0, A.add)
+        tt(lg(DQ), q2, q1, A.subtract)
+        tt(lg(DP), q1, b("P0"), A.subtract)
+        for e in range(1, 7):
+            if e == 6: partial(t)
+            for z in "AB":
+                back(t, e, z)
+                if e < 6: front(t, e + 1, z)
+        if t: give_back(t)
+        acc(SA, 16, 6)
+        ts(lg(FO), lg(SA), 3520, A.not_equal)
+        if t < 2: send(t)
+        adopt(t)
+        if t < 2:
+            if t: get_back(t)
+            recount()
+        write_men(t)
+        if t == 2:
+            fill(b("F1", M, M + 16), 0.0)
+            fill(b("F2", M, M + 16), 0.0)
+            fill(b("X", M, M + 16), 0.0)
+            dma("s", T.fo[:, 0:M], (T.F1[0:128:16, 0:M], [("F1", 0, M)]), "st1")
+            dma("y", T.f2o[:, 0:M], (T.F2[0:128:16, 0:M], [("F2", 0, M)]), "st2")
+            get_back(t)
+            new_men(t)
+    dma("y", T.xo[:, M:W], b("X", M, W), "st3")
+    dma("s", T.fo[:, M:W], (T.F1[0:128:16, M:W], [("F1", M, W)]), "st4")
+    dma("y", T.f2o[:, M:W], (T.F2[0:128:16, M:W], [("F2", M, W)]), "st5")
+    for sem, val in count.items():
+        if know["g"].get(sem, 0) < val:
+            g.wait_ge(T.sem[sem], val)
+            know["g"][sem] = val

@@ -2,7 +2,7 @@ from concourse.mybir import dt, AluOpType as A, AxisListType, ActivationFunction
 
 M, W, WX, EMPTY, EXT = 3520, 3664, 3920, 3520, 3856
 NB = 229
-KS = [[2, 2, 2, 2, 2, 2], [4, 4, 4, 3, 3, 3]]
+KS = [[3, 3, 3, 2, 2, 2], [4, 4, 4, 4, 4, 4]]
 
 _sb = {
     "SI": (3520, "int32"), "SN": (WX, "float32"), "X": (WX, "bfloat16"), "F1": (WX, "float32"), "F2": (WX, "float32"),
@@ -32,7 +32,10 @@ _sb = {
     "EZY": (192, "float32"), "EZS": (192, "float32"), "YX": (192, "float32"), "SX": (192, "float32"), "YM": (192, "float32"), "SM": (192, "float32"),
     "DGY": (192, "bfloat16"), "DGS": (192, "bfloat16"), "EBY": (1056, "bfloat16"), "EBS": (1056, "bfloat16"), "SY": (192, "float32"),
     "NY": (192, "bfloat16"), "EA": (192, "bfloat16"), "FF": (192, "float32"), "DS": (192, "float32"), "NC": (192, "float32"),
-    "SHA": (128, "float32"), "SHB": (128, "float32"), "HV": (192, "float32"), "MI": (192, "int32"), "MJ": (192, "int32"), "CC": (64, "float32"), "RT": (16, "float32"), "RLU": (16, "uint16"),
+    "ZD1": (32, "float32"), "ZD2": (32, "float32"), "W1": (32, "float32"), "W2": (32, "float32"), "W3": (32, "float32"), "GEM": (64, "float32"),
+    "D16": (16, "float32"), "T64": (64, "float32"), "T32": (32, "float32"), "T16": (16, "float32"), "E16": (16, "float32"), "VAL": (48, "float32"),
+    "GO2": (24, "float32"), "SV2": (24, "float32"), "JK2": (24, "float32"), "L24": (24, "float32"), "M24": (24, "float32"), "NSL": (12, "float32"),
+    "EBT": (1056, "bfloat16"), "NBO": (128, "bfloat16"), "LM": (192, "bfloat16"), "SHA": (128, "float32"), "SHB": (128, "float32"), "HV": (192, "float32"), "MI": (192, "int32"), "MJ": (192, "int32"), "CC": (64, "float32"), "RT": (16, "float32"), "RLU": (16, "uint16"),
 }
 _apart = ("GC", "FC", "WT", "REP", "LQ", "LQQ", "LW")
 AT, _used = {}, {}
@@ -46,7 +49,8 @@ SCRATCH = {k: ("sbuf", [128, n], d) for k, (n, d) in _sb.items() if AT[k][0] == 
 for _d, _n in _used.items(): SCRATCH["all_" + _d] = ("sbuf", [128, _n], _d)
 for _n in ("D3A", "D3B"): SCRATCH[_n] = ("sbuf", [128, 8, 256], "bfloat16")
 for _n in ("SGA", "SGB"): SCRATCH[_n] = ("sbuf", [128, 4, 32], "float32")
-for _n in ("PY0", "PY1", "LX1", "LX2", "RS1", "RS2", "RL1", "RL2"): SCRATCH[_n] = ("sbuf", [128, 72], "bfloat16")
+for _n in ("PY0", "PY1", "LX1", "LX2"): SCRATCH[_n] = ("sbuf", [128, 80], "bfloat16")
+for _n in ("RS1", "RS2", "RL1", "RL2"): SCRATCH[_n] = ("sbuf", [128, 72], "bfloat16")
 for _n in ("KEYA", "KEYB", "SUB0", "SUB1", "M0", "M1"): SCRATCH[_n] = ("psum", [128, 512], "float32")
 for _n in ("PWA", "PWB"): SCRATCH[_n] = ("psum", [128, 16, 32], "float32")
 PSUM = {k for k, v in SCRATCH.items() if v[0] == "psum"}
@@ -165,7 +169,7 @@ def rank_program(g, core, T, topo):
     def remote(to, dst, src, rsem, lsem):
         peer = T.cores[to]
         deps = set()
-        need("g", (src, 0, 72), False, deps)
+        need("g", (src, 0, 80), False, deps)
         waits("g", deps)
         rid, pid, _ = topo.addr(peer)
         n = len(topo.engines(core, peer))
@@ -178,7 +182,7 @@ def rank_program(g, core, T, topo):
         n = len(topo.engines(T.cores[frm], core))
         count[sem] = n
         clocks[(sem, n)] = {}
-        book("rem", (buf, 0, 72), True, (sem, n))
+        book("rem", (buf, 0, 80), True, (sem, n))
 
     dma("y", b("GC", p=88), T.gn[:], "ld0")
     dma("y", b("FC", p=88), T.fa[:], "ld1")
@@ -224,9 +228,14 @@ def rank_program(g, core, T, topo):
         num(b("EQ" + k), 128, 0)
     for k in "12":
         num(b("UP" + k), 16, 3520)
+    for k in "12":
+        num(b("ZD" + k, 0, 16), 16, 0)
+    gop(ia, b("HI"), [], [[[0, 112]], 0, 0])
     for k in "01":
         num(b("SR" + k, 0, 64), 64, 3520)
-    for n in ("PY0", "PY1", "RS1", "RS2"): num(b(n, 64, 72), 8, 0)
+        num(b("PY" + k, 64, 80), 16, 0)
+    for n in ("RS1", "RS2"): num(b(n, 64, 72), 8, 0)
+    gop(ia, b("LM"), [], [[[1, 12], [0, 16]], 0, 0], allow_small_or_imprecise_dtypes=True)
     num(b("ADD"), WX, 0)
 
     cp(b("GB", p=88), b("GC", p=88))
@@ -239,13 +248,17 @@ def rank_program(g, core, T, topo):
         k = banks[r % 4]
         mm(b(k, 0, 320), b("REP", 128 * r, 128 * r + 128, p=88), b("GB", p=88), True, True)
         act(b("GNR", 320 * r, 320 * r + 320), b(k, 0, 320), F.Copy)
+    fbank = ["M0", "M1", "SUB0", "SUB1", "M0", "M1", "KEYA", "KEYB", "SUB0", "SUB1", "M1"]
     for r in range(11):
-        k = banks[(r + 3) % 4]
+        k = fbank[r]
         rep = b("REP", 128 * r, 128 * r + 128, p=88)
         mm(b(k, 0, 320), rep, b("FB", 0, 320, p=88), True, False)
         mm(b(k, 0, 320), rep, b("FB", 320, 640, p=88), False, True)
-        act(b("F1", 320 * r, 320 * r + 320), b(k, 0, 320), F.Copy)
-    dma("y", b("F2", 0, M), b("F1", 0, M), "cp0")
+        if r < 6: act(b("F1", 320 * r, 320 * r + 320), b(k, 0, 320), F.Copy)
+
+    def more_fathers():
+        for r in range(6, 11): cp(b("F1", 320 * r, 320 * r + 320), b(fbank[r], 0, 320))
+        dma("y", b("F2", 0, M), b("F1", 0, M), "cp0")
     ts(b("PQ", 0, 1), b("PI"), 15, A.bitwise_and)
     ts(b("PQ", 1, 2), b("PI"), 16, A.bitwise_and)
     QC, I4, E0, C0, N1c, E1c, H0, H1, Q16, W16, QP = [c1("COL", j) for j in range(11)]
@@ -283,6 +296,7 @@ def rank_program(g, core, T, topo):
     ts(b("IP"), b("IP"), 15, A.bitwise_and)
     ts(b("MASK"), b("IP"), 0, A.is_equal)
     ts(b("RES"), b("L15"), 0, A.not_equal)
+    more_fathers()
     def late_constants():
         ts(b("RESB"), b("RES"), -1e7, A.mult, 1e7, A.add)
         ts(b("NEGI"), b("IDN"), -1.0, A.mult)
@@ -296,6 +310,8 @@ def rank_program(g, core, T, topo):
     def later_constants():
         ts(W16, b("WT"), 0.0625, A.mult)
         ts(b("LW"), b("LQ"), W16, A.mult)
+        ts(b("NBO"), b("BO"), -1.0, A.mult)
+        for j in (0, 12): cp(b("JK2", j, j + 12), b("JK"))
         ts(QP, b("PQ", 0, 1), 1.0, A.add)
         for k in "YS":
             ts(b("EZ" + k), b("L15", 0, 192), QP, A.is_equal, -20000.0, A.mult)
@@ -303,6 +319,11 @@ def rank_program(g, core, T, topo):
         ts(b("TRI2"), b("TRI"), 2.0, A.mult)
         tt(b("TRI2"), b("TRI2"), b("IDN"), A.subtract)
         ts(b("NEWT"), b("I1", 0, 64), 3536.0, A.add, E1c, A.mult)
+
+    def weave(*parts):
+        parts = [iter(p) for p in parts]
+        while parts:
+            parts = [p for p in parts if next(p, p) is not p]
 
     def lg(j, n=12, lo=0): return b("LG", 12 * j + lo, 12 * j + lo + n)
 
@@ -318,7 +339,7 @@ def rank_program(g, core, T, topo):
 
     def lanes(t, meanwhile):
         r = 107 * t % NB
-        sign = 9 if t else 10
+        sign = 10
         if t == 0:
             ts(b("OKR", 0, 220), b("M0", 0, 220), 0, A.is_equal)
             ts(b("NOK", 0, 220), b("M0", 0, 220), 0, A.not_equal)
@@ -334,6 +355,11 @@ def rank_program(g, core, T, topo):
         for m in range(sign, 12):
             ts(b("CM%d" % (m % 2), 0, NB), b("SB", 0, NB), c1("BJ", m), A.is_le)
             call("v", V.tensor_reduce, c1("KA", m), [b("CM%d" % (m % 2), 0, NB)], [AxisListType.X, A.add], {})
+        if t:
+            LX = "LX%d" % t
+            arrive((rank - t) % N, LX, "snd_in%d" % (t - 1))
+            act(b("XLR", 0, 512), ind(LX, b("ARO", 0, 32), hi=64), F.Copy)
+            act(b("XLR", 3584, 4096), ind(LX, b("ARO", 32, 64), hi=64), F.Copy)
         meanwhile()
         ts(b("KA", 0, sign), b("KA", 0, sign), 0.5, A.mult, NB / 2.0, A.add)
         cp(b("KO"), b("KA"))
@@ -350,11 +376,17 @@ def rank_program(g, core, T, topo):
 
     def climb(F_, src, out):
         ts(b("PX"), src, 64, A.is_lt, float(EXT), A.mult)
+        yield
         tt(b("PX"), b("PX"), src, A.add)
+        yield
         cp(b("PU"), b("PX"))
+        yield
         tt(b("G1"), ind(F_, b("PU")), b("MASK", 0, 192), A.mult)
+        yield
         scan(b("G2"), b("RES", 0, 192), b("G1"), 0.0, A.mult, A.add)
+        yield
         cp(out, b("G2", 15, 192, 16))
+        yield
 
     def starts(t):
         F_ = "F2" if t % 2 else "F1"
@@ -369,23 +401,16 @@ def rank_program(g, core, T, topo):
             LX = "LX%d" % t
             for q in range(16):
                 mm(b("M1", 0, 4), lq(q, "LW"), b(LX, q, 64, 16), q == 0, q == 15)
-            act(b("XLR", 0, 512), ind(LX, b("ARO", 0, 32), hi=64), F.Copy)
             cp(b("HI", 0, 4), b("M1", 0, 4))
             ts(b("HI", 0, 4), b("HI", 0, 4), 63, A.bitwise_and)
-            ts(b("AL", 0, 4), b(LX, 64, 68), 3, A.is_lt)
-            ts(b("AL", 4, 8), b("HI", 0, 4), -1.0, A.mult, 3520.0, A.add)
-            tt(b("AL", 4, 8), b("AL", 4, 8), b("AL", 0, 4), A.mult)
-            tt(b("AL", 4, 8), b("AL", 4, 8), b("HI", 0, 4), A.add)
-            cp(b("CU", 0, 2), b("AL", 4, 6))
-            cp(b("CU", 14, 16), b("AL", 6, 8))
+            cp(b("CU", 0, 2), b("HI", 0, 2))
+            cp(b("CU", 14, 16), b("HI", 2, 4))
 
     def starts_a(t):
         cp(b("XLR", 512, 1280), ind("X", b("HRU", 0, 48)))
 
     def starts_b(t):
         act(b("XLR", 2048, 3584), ind("X", b("HRU", 96, 192)), F.Copy)
-        if t:
-            act(b("XLR", 3584, 4096), ind("LX%d" % t, b("ARO", 32, 64), hi=64), F.Copy)
 
     def hist(e, lo, hi): return b("HI", 16 * e + lo, 16 * e + hi)
 
@@ -393,7 +418,7 @@ def rank_program(g, core, T, topo):
         if z == "A": return (0 if t else 2), 8, 2, 8
         return 8, (16 if t else 14), 8, 14
 
-    Z1, Z2, REAL, DQ, DP, ALB, TA, TB, SA, YA, MA, FO, MB = range(13)
+    TC, REAL, DQ, DP, ALB, TA, TB, FO, YLs = range(9)
     UP = {1: "UP1", 2: "UP2"}
 
     def front(t, e, z, between=None, behind=None):
@@ -406,9 +431,8 @@ def rank_program(g, core, T, topo):
         su, df, xg, sg, dd, pw, key = "SU" + z, "DF" + z, "XG" + z, "SG" + z, "D3" + z, "PW" + z, "KEY" + z
         sub = ("SUB0", "M0") if z == "A" else ("SUB1", "M1")
         nb = kc // 2
-        act(b("SH" + z, 0, n), ind("SN", cu), F.Identity, bias=I4)
         cp(b(su, 0, n), ind("SN", cu))
-        act(d3(sg, 0, nb), b("SH" + z, 0, n), F.Copy)
+        ts(d3(sg, 0, nb), b(su, 0, n), I4, A.add)
         if between: between()
         for P in (0, 1):
             mm(d3(pw, 0, nb, 16 * P, 16 * P + 16), b("QD%d" % P), d3(sg, 0, nb, 16 * P, 16 * P + 16), True, False)
@@ -417,9 +441,9 @@ def rank_program(g, core, T, topo):
         if behind: behind()
         x0 = 256 * k0
         c4 = min(kv, 4)
-        tt(b(df, 0, 256 * c4), ind("X", b(su, 0, 16 * c4)), b("XLR", x0, x0 + 256 * c4), A.subtract)
-        if kv > 4:
-            tt(b(df, 1024, 256 * kv), ind("X", b(su, 64, 16 * kv)), b("XLR", x0 + 1024, x0 + 256 * kv), A.subtract)
+        for lo, hi in [(0, c4)] + ([(4, kv)] if kv > 4 else []):
+            tt(b(df, 256 * lo, 256 * hi), ind("X", b(su, 16 * lo, 16 * hi)), b("XLR", x0 + 256 * lo, x0 + 256 * hi), A.subtract)
+            yield
         subs = [(kv + 2 * j, min(kv + 2 * j + 2, kc), sub[j]) for j in range((ks + 1) // 2)]
         for lo, hi, bank in subs:
             w = 256 * (hi - lo)
@@ -436,24 +460,28 @@ def rank_program(g, core, T, topo):
             m0, m1 = o0 - 2, o1 - 2
             ex = b("EX" + z, 16 * i0, 16 * i1, 16)
             L = m1 - m0
-            my, ta, tb = "MX" + z, lg(TA, L, m0), lg(TB, L, m0)
+            my, ta = "MX" + z, lg(TA, L, m0)
             if e == 1:
                 ts(ex, b("H", m0, m1), 4096.0, A.add)
             else:
-                Z = lg(Z1 if e == 2 else Z2, L, m0)
+                Z = b("ZD%d" % (e - 1), o0, o1)
                 ts(Z, b(my, 16 * i0 + 15, 16 * i1, 16), 4096, A.is_lt)
                 tt(ta, Z, b("P0P", m0, m1) if e == 2 else lg(ALB, L, m0), A.mult)
-                if e == 2:
-                    tt(tb, Z, lg(DQ, L, m0), A.mult)
+                if e == 2 and z == "B":
+                    tt(lg(TB), b("ZD1", 2, 14), lg(DQ), A.mult)
                 ts(ex, ta, 4095.0, A.add)
-                if e == 2:
-                    tt(b("UP2", o0, o1), tb, b("UP1", o0, o1), A.add)
-                    tt(ta, Z, lg(DP, L, m0), A.mult)
-                    tt(lg(ALB, L, m0), ta, b("P0P", m0, m1), A.add)
+                if e == 2 and z == "B":
+                    tt(b("UP2", 2, 14), lg(TB), b("UP1", 2, 14), A.add)
+                    tt(lg(TC), b("ZD1", 2, 14), lg(DP), A.mult)
+                    tt(lg(ALB), lg(TC), b("P0P"), A.add)
+            yield
             scan(b("BX" + z, 16 * i0, 16 * i1), b("RES", 0, 16 * L), b("EX" + z, 16 * i0, 16 * i1), 0.0, A.mult, A.add)
+            yield
         call("v", V.transpose, sig, [d3(pw, 0, nb)], [], {})
+        yield
         if e <= 3:
             tt(b("EQ" + z, 16 * i0, 16 * i1), b("SIG" + z, 16 * i0, 16 * i1), b("BX" + z, 16 * i0, 16 * i1), A.is_equal)
+            yield
         for lo, hi in ((0, c4), (c4, kc)):
             o = b(key, 16 * lo, 16 * hi)
             mm(o, b("IDN"), b("SLOT", 16 * lo, 16 * hi), True, False)
@@ -471,109 +499,162 @@ def rank_program(g, core, T, topo):
         key, pm, fe, mx, sx = b("KEY" + z, 0, n), b("PM" + z, 0, n), b("FE" + z, 0, n), b("MX" + z, 0, n), b("SX" + z, 0, kc)
         if e <= 3: scan(pm, b("RES", 0, n), key, 0.0, A.mult, A.min)
         else: scan(pm, b("RESB", 0, n), key, 1e7, A.add, A.min)
+        yield
         tt(fe, key, pm, A.is_equal)
+        yield
         tt(fe, fe, b("SIG" + z, 0, n), A.mult)
+        yield
         f0 = b("FE" + z, 0, n, 16)
         if e <= 2: tt(f0, f0, b(UP[e], k0, k1), A.max)
         elif e == 3: ts(f0, f0, 3520, A.max)
+        if e <= 3: yield
         scan(mx, b("RES", 0, n), fe, 0.0, A.mult, A.max)
+        yield
         cp(sx, b("MX" + z, 15, n, 16))
+        yield
         ts(hist(e, k0, k1), sx, 4095, A.bitwise_and)
+        yield
         if e < 6:
             cp(b("CU", k0, k1), hist(e, k0, k1))
 
-    def acc(dst, m, e, first=False):
-        tt(lg(TB), lg(m), hist(e, 2, 14), A.mult)
-        tt(lg(dst), lg(dst), lg(TB), A.add)
-
-    def arr(e):
-        LXg = b("GE", 4 * (e - 3), 4 * (e - 3) + 4)
-        tt(b("AL", 12, 14), b("GE", 4 * (e - 3), 4 * (e - 3) + 2), hist(e, 0, 2), A.mult)
-        tt(b("AL", 14, 16), b("GE", 4 * (e - 3) + 2, 4 * (e - 3) + 4), hist(e, 14, 16), A.mult)
-        if e == 3: ts(b("AL", 16, 20), b("AL", 0, 4), 3520.0, A.mult)
-        tt(b("AL", 16, 20), b("AL", 16, 20), b("AL", 12, 16), A.add)
+    def pair(e): return b("HI", 16 * e - 16, 16 * e + 16)
+    YA, SA = b("W1", 2, 14), b("W1", 18, 30)
 
     def partial(t):
-        ts(lg(MA), lg(Z1), -1.0, A.mult, 1.0, A.add)
-        ts(lg(MB), lg(Z2), -1.0, A.mult, 1.0, A.add)
-        tt(lg(13), lg(MA), lg(MB), A.mult)
-        tt(lg(14), lg(Z1), lg(MB), A.mult)
-        tt(lg(15), lg(MA), lg(Z2), A.mult)
-        tt(lg(16), lg(Z1), lg(Z2), A.mult)
-        tt(lg(SA), lg(13), hist(2, 2, 14), A.mult)
-        tt(lg(YA), lg(13), hist(1, 2, 14), A.mult)
-        acc(SA, 14, 4)
-        acc(YA, 14, 3)
-        acc(SA, 15, 5)
-        acc(YA, 15, 4)
-        acc(YA, 16, 5)
+        for k in "12": cp(b("ZD" + k, 16, 32), b("ZD" + k, 0, 16))
+        w1, w2, w3, z1, z2 = b("W1"), b("W2"), b("W3"), b("ZD1"), b("ZD2")
+        tt(w1, pair(4), pair(2), A.subtract)
+        yield
+        tt(w3, z1, z2, A.mult)
+        yield
+        tt(w1, w1, z1, A.mult)
+        tt(w2, z2, w3, A.subtract)
+        yield
+        tt(w1, w1, pair(2), A.add)
+        tt(w2, w2, pair(5), A.mult)
+        yield
+        tt(b("T32"), w1, z2, A.mult)
+        yield
+        tt(w1, w1, w2, A.add)
+        yield
+        tt(w1, w1, b("T32"), A.subtract)
+        yield
         if t:
+            lx = b("LX%d" % t, 64, 80)
             for e in (3, 4, 5, 6):
-                ts(b("GE", 4 * (e - 3), 4 * (e - 3) + 4), b("LX%d" % t, 64, 68), e, A.is_equal)
-            for e in (3, 4, 5): arr(e)
+                ts(b("GEM", 16 * e - 48, 16 * e - 32), lx, e, A.is_equal)
+            ts(b("D16"), lx, 3, A.is_lt, 3520.0, A.mult)
+
+    def own_found():
+        tt(b("W2"), b("W3"), pair(6), A.mult)
+        yield
+        tt(b("W1"), b("W1"), b("W2"), A.add)
+        yield
+        ts(lg(FO), SA, 3520, A.not_equal)
 
     def give_back(t):
         rs = "RS%d" % t
-        arr(6)
-        ts(b("AL", 20, 24), b("AL", 16, 20), 3520, A.is_equal)
-        ts(b(rs, 64, 68), b("AL", 16, 20), 3520, A.not_equal)
-        tt(b("AL", 24, 28), b("AL", 16, 20), b("AL", 20, 24), A.add)
-        cp(b("RU"), b("AL", 24, 28))
+        t16 = b("T16")
+        tt(b("T64"), b("GEM"), b("HI", 48, 112), A.mult)
+        yield
+        tt(b("T32"), b("T64", 0, 32), b("T64", 32, 64), A.add)
+        yield
+        tt(t16, b("T32", 0, 16), b("T32", 16, 32), A.add)
+        yield
+        tt(t16, t16, b("D16"), A.add)
+        yield
+        ts(b("E16"), t16, 3520, A.is_equal)
+        tt(b("E16"), b("E16"), t16, A.add)
+        cp(b("RU", 0, 2), b("E16", 0, 2))
+        cp(b("RU", 2, 4), b("E16", 14, 16))
+        ts(b(rs, 64, 66), b("T16", 0, 2), 3520, A.not_equal)
+        ts(b(rs, 66, 68), b("T16", 14, 16), 3520, A.not_equal)
         cp(b(rs, 0, 64), ind("X", b("RU")))
         remote((rank - t) % N, "RL%d" % t, rs, "ret_in%d" % t, "ret_out%d" % t)
 
     def send(t):
         py, SE = "PY%d" % t, b("SENT", 4 * t, 4 * t + 4)
         tt(b("LO"), lg(REAL), lg(FO), A.subtract)
-        mm(b("M1", 0, 12), b("BO"), b("LO"), True, True)
-        mm(b("M1", 16, 28), b("TM"), b("LO"), True, True)
-        scan(lg(TA), b("ONEF", 0, 12), b("M1", 0, 12), 0.0, A.mult, A.add)
-        tt(lg(TA), b("M1", 16, 28), lg(TA), A.add)
-        tt(lg(TA), lg(TA), b("JS"), A.subtract)
-        tt(lg(TA), lg(TA), b("LO"), A.mult)
-        tt(lg(TA), lg(TA), b("JS"), A.add)
-        cp(b("SLU"), lg(TA))
+        mm(b("KEYA", 0, 12), b("BO"), b("LO"), True, True)
+        mm(b("KEYA", 16, 28), b("TM"), b("LO"), True, True)
+        yield
+        scan(lg(TC), b("ONEF", 0, 12), b("KEYA", 0, 12), 0.0, A.mult, A.add)
+        yield
+        tt(lg(TC), b("KEYA", 16, 28), lg(TC), A.add)
+        yield
+        tt(lg(TC), lg(TC), b("JS"), A.subtract)
+        yield
+        tt(lg(TC), lg(TC), b("LO"), A.mult)
+        yield
+        tt(lg(TC), lg(TC), b("JS"), A.add)
+        yield
+        cp(b("SLU"), lg(TC))
+        yield
         sr = "SR%d" % t
         w = ind(sr, b("SLU"), hi=384)
         cp(w, b("HREP"))
-        diag(b("S4U"), b(sr, 0, 64), 64, "G4", "G5")
-        cp(SE, b("S4U"))
-        cp(b(py, 0, 64), ind("X", b("S4U")))
-        tt(b("G4"), ind("GNR", b("S4U"), hi=W), b("MASK", 0, 64), A.mult)
+        yield
+        tt(b("G4"), b(sr, 0, 64), b("MASK", 0, 64), A.mult)
+        yield
         scan(b("G5"), b("RES", 0, 64), b("G4"), 0.0, A.mult, A.add)
-        cp(b(py, 64, 68), b("G5", 15, 64, 16))
+        yield
+        cp(b("S4U"), b("G5", 15, 64, 16))
+        cp(SE, b("G5", 15, 64, 16))
+        yield
+        tt(b("G4"), ind("GNR", b("S4U"), hi=W), b("MASK", 0, 64), A.mult)
+        yield
+        cp(b(py, 0, 64), ind("X", b("S4U")))
+        scan(b("G5"), b("RES", 0, 64), b("G4"), 0.0, A.mult, A.add)
+        yield
+        cp(b(py, 64, 66), b("G5", 15, 32, 16))
+        cp(b(py, 78, 80), b("G5", 47, 64, 16))
         remote((rank + 1 + t) % N, "LX%d" % (t + 1), py, "snd_in%d" % t, "snd_out%d" % t)
-
-    def choose(out, base, cond, val):
-        tt(lg(TA), val, base, A.subtract)
-        tt(lg(TA), lg(TA), cond, A.mult)
-        tt(out, lg(TA), base, A.add)
 
     def adopt(t):
         last = t == 2
-        YL, SL, GO, SV, LT = lg(13), lg(SA), lg(15), lg(16), lg(17)
+        YL, SL, go = lg(YLs), SA, b("GO2", 0, 12)
         cp(b("LU", 12, 24), SL)
         act(b("SREP"), ind("IOTA", b("LU", 12, 24)), F.Copy)
-        ts(lg(TA), lg(YA), -3520.0, A.add)
+        ts(lg(TA), YA, -3520.0, A.add)
+        yield
+        ts(b("NSL"), SL, -1.0, A.mult)
+        yield
         tt(lg(TA), lg(TA), lg(FO), A.mult)
-        ts(YL, lg(TA), 3520.0, A.add)
-        cp(b("LU", 0, 12), YL)
-        act(b("YREP"), ind("IOTA", b("LU", 0, 12)), F.Copy)
-        tt(b("MI"), ind("X", b("LU", 12, 24)), b("XLR", 512, 3584, 16), A.add)
-        ts(b("EZY", 0, 192, 16), YL, 20000.0, A.add)
-        scan(b("YX"), b("RES", 0, 192), b("EZY"), 0.0, A.mult, A.add)
-        ts(b("EZS", 0, 192, 16), SL, 20000.0, A.add)
-        scan(b("SX"), b("RES", 0, 192), b("EZS"), 0.0, A.mult, A.add)
         off = [0]
         for k in range(11): off.append(off[-1] + 176 - 16 * k)
-        for nm, li, st in (("S", SA, True), ("Y", 13, False)):
-            rep = nm + "REP"
-            tt(b("DG" + nm), b(rep), b(nm + "X"), A.is_equal)
-            for k in range(11):
-                ts(b("EB" + nm, off[k], off[k + 1]), b(rep, 16 * k + 16, 192), b("LG", 12 * li + k, 12 * li + k + 1), A.is_equal)
-            mm(b("M1", 0, 192), b("BO"), b("DG" + nm), st, False)
-            for k in range(11):
-                mm(b("M1", 16 * k + 16, 192), b("BO"), b("EB" + nm, off[k], off[k + 1]), False, k == 10 and not st)
+        for lo, hi in ((0, 4), (4, 11)):
+            for k in range(lo, hi):
+                act(b("EBS", off[k], off[k + 1]), b("SREP", 16 * k + 16, 192), F.Sign, bias=c1("NSL", k))
+            act(b("EBT", off[lo], off[hi]), b("EBS", off[lo], off[hi]), F.Abs)
+        yield
+        ts(YL, lg(TA), 3520.0, A.add)
+        yield
+        cp(b("LU", 0, 12), YL)
+        yield
+        ts(b("EZS", 0, 192, 16), SL, 20000.0, A.add)
+        yield
+        cp(b("YREP"), ind("IOTA", b("LU", 0, 12)))
+        yield
+        scan(b("SX"), b("RES", 0, 192), b("EZS"), 0.0, A.mult, A.add)
+        yield
+        ts(b("EZY", 0, 192, 16), YL, 20000.0, A.add)
+        yield
+        tt(b("MI"), ind("X", b("LU", 12, 24)), b("XLR", 512, 3584, 16), A.add)
+        yield
+        scan(b("YX"), b("RES", 0, 192), b("EZY"), 0.0, A.mult, A.add)
+        yield
+        for k in range(11):
+            ts(b("EBY", off[k], off[k + 1]), b("YREP", 16 * k + 16, 192), c1("LG", 12 * YLs + k), A.is_equal)
+            yield
+        tt(b("DGY"), b("YREP"), b("YX"), A.is_equal)
+        tt(b("DGS"), b("SREP"), b("SX"), A.is_equal)
+        mm(b("M1", 0, 192), b("BO"), b("LM"), True, False)
+        mm(b("M1", 0, 192), b("BO"), b("DGY"), False, False)
+        for k in range(11):
+            mm(b("M1", 16 * k + 16, 192), b("BO"), b("EBY", off[k], off[k + 1]), False, False)
+        mm(b("M1", 0, 192), b("BO"), b("DGS"), False, False)
+        for k in range(11):
+            mm(b("M1", 16 * k + 16, 192), b("NBO"), b("EBT", off[k], off[k + 1]), False, k == 10)
         cp(b("SY"), ind("SN", b("LU", 0, 12)))
         ts(b("NY"), b("SY"), 3520, A.not_equal)
         for q in range(16):
@@ -582,39 +663,42 @@ def rank_program(g, core, T, topo):
             tt(b("EA"), b("SY"), b("SREP"), A.is_equal)
             mm(b("SUB0", 0, 192), b("TRI2"), b("EA"), True, True)
             act(b("DS"), b("SREP"), F.Copy, bias=3520.0, scale=-1.0)
+        jk = b("JK")
+        tt(b("VAL", 0, 12), SL, jk, A.subtract)
+        tt(b("VAL", 12, 24), b("H"), jk, A.subtract)
+        tt(b("VAL", 24, 36), YL, jk, A.subtract)
+        tt(b("VAL", 36, 48), SL, jk, A.subtract)
+        ts(b("MJ"), b("MI"), 1, A.arith_shift_right)
         tt(b("G1"), b("M1", 0, 192), b("MASK", 0, 192), A.mult)
         scan(b("G2"), b("RES", 0, 192), b("G1"), 0.0, A.mult, A.add)
-        ts(GO, b("G2", 15, 192, 16), 0, A.is_equal)
-        tt(GO, GO, lg(FO), A.mult)
+        ts(b("M24", 0, 12), b("G2", 15, 192, 16), 0, A.is_equal)
+        tt(go, b("M24", 0, 12), lg(FO), A.mult)
+        tt(b("GO2", 12, 24), b("M24", 0, 12), lg(FO), A.mult)
+        targets(24, "GO2", 0)
         if not last:
-            choose(LT, b("JK"), GO, b("H"))
-            cp(b("LU", 36, 48), LT)
             cp(ind("ADD", b("LU", 36, 48)), b("ONES", 0, 192))
+
+    def targets(at, cond, v):
+        tt(b("L24"), b(cond), b("VAL", v, v + 24), A.mult)
+        tt(b("L24"), b("L24"), b("JK2"), A.add)
+        cp(b("LU", at, at + 24), b("L24"))
 
     def write_men(t):
         last = t == 2
-        YL, SL, GO, SV, LT = lg(13), lg(SA), lg(15), lg(16), lg(17)
-        ts(b("MJ"), b("MI"), 1, A.arith_shift_right)
-        choose(LT, b("JK"), GO, SL)
-        cp(b("LU", 24, 36), LT)
         cp(ind("X", b("LU", 24, 36)), b("MJ"))
         if last: dma("y", T.xo[:, 0:M], b("X", 0, M), "st0")
-        ts(SV, b("SUB1", 0, 12), 24, A.is_gt)
-        tt(SV, SV, GO, A.mult)
+        ts(b("M24", 0, 12), b("SUB1", 0, 12), 24, A.is_gt)
+        for j in (0, 12): tt(b("SV2", j, j + 12), b("M24", 0, 12), b("GO2", 0, 12), A.mult)
         cp(ind("F2", b("LU", 24, 36)), b("HREP"))
-        choose(LT, b("JK"), SV, SL)
-        cp(b("LU", 60, 72), LT)
+        targets(48, "SV2", 24)
         cp(ind("F1", b("LU", 60, 72)), b("HREP"))
 
     def write_sons(t):
-        YL, SV, LT = lg(13), lg(16), lg(17)
         ts(b("HV"), b("SREP"), E0, A.mult, C0, A.add)
         cp(ind("SN", b("LU", 36, 48)), b("HV"))
         ts(b("FF"), b("SUB0", 0, 192), -1, A.is_equal)
         tt(b("FF"), b("FF"), b("DS"), A.mult)
         tt(b("NC"), b("FF"), b("SY"), A.add)
-        choose(LT, b("JK"), SV, YL)
-        cp(b("LU", 48, 60), LT)
         cp(ind("SN", b("LU", 48, 60)), b("NC"))
         if t == 1:
             ts(b("CC"), ind("SN", b("RLU", 4, 8)), N1c, A.mult)
@@ -648,29 +732,26 @@ def rank_program(g, core, T, topo):
     for t in range(3):
         lanes(t, (lambda: rest(t - 1)) if t else late_constants)
         ts(lg(REAL), b("H"), 3520, A.not_equal)
-        if t:
-            arrive((rank - t) % N, "LX%d" % t, "snd_in%d" % (t - 1))
         starts(t)
         F_ = "F2" if t % 2 else "F1"
         q1, q2 = b("UP1", 2, 14), b("Q2")
-        front(t, 1, "A", lambda: starts_a(t), lambda: starts_b(t))
-        front(t, 1, "B", None if t else later_constants)
+
+        def climbs():
+            yield from climb(F_, b("P0"), q1)
+            ts(b("P0P"), b("P0"), 1.0, A.add)
+            yield from climb(F_, q1, q2)
+            tt(lg(DQ), q2, q1, A.subtract)
+            tt(lg(DP), q1, b("P0"), A.subtract)
+        weave(front(t, 1, "A", lambda: starts_a(t), lambda: starts_b(t)))
+        weave(front(t, 1, "B", None if t else later_constants), climbs())
         act(b("HREP"), ind("IOTA", b("HU")), F.Copy)
-        climb(F_, b("P0"), q1)
-        climb(F_, q1, q2)
-        ts(b("P0P"), b("P0"), 1.0, A.add)
-        tt(lg(DQ), q2, q1, A.subtract)
-        tt(lg(DP), q1, b("P0"), A.subtract)
-        for e in range(1, 7):
-            if e == 6: partial(t)
-            for z in "AB":
-                back(t, e, z)
-                if e < 6: front(t, e + 1, z)
-        if t: give_back(t)
-        acc(SA, 16, 6)
-        ts(lg(FO), lg(SA), 3520, A.not_equal)
-        if t < 2: send(t)
-        adopt(t)
+        weave(back(t, 1, "A"))
+        for e in range(2, 7):
+            weave(front(t, e, "A"), back(t, e - 1, "B"))
+            weave(front(t, e, "B"), back(t, e, "A"))
+        weave(back(t, 6, "B"), partial(t))
+        weave(give_back(t) if t else [], own_found())
+        weave(adopt(t), send(t) if t < 2 else [])
         if t < 2:
             if t: get_back(t)
             recount()

@@ -2,6 +2,7 @@ from concourse.mybir import dt, AluOpType as A, AxisListType, ActivationFunction
 
 M, W, WX, EMPTY, EXT = 3520, 3664, 3920, 3520, 3856
 NB = 229
+SIGN = [10, 10]
 KS = [[3, 3, 3, 2, 2, 2], [4, 4, 4, 4, 4, 4]]
 
 _sb = {
@@ -23,7 +24,7 @@ _sb = {
     "HRU": (192, "uint16"), "XLR": (4096, "bfloat16"), "G1": (192, "float32"), "G2": (192, "float32"), "P0": (12, "float32"),
     "P0P": (12, "float32"), "Q1": (12, "float32"), "Q2": (12, "float32"), "PX": (12, "float32"), "PU": (12, "uint16"), "CU": (16, "uint16"),
     "SUA": (128, "uint16"), "SUB": (128, "uint16"), "DFA": (2048, "bfloat16"), "DFB": (2048, "bfloat16"), "XGA": (1024, "bfloat16"),
-    "XGB": (1024, "bfloat16"), "SIGA": (128, "float32"), "SIGB": (128, "float32"), "EXA": (128, "float32"), "EXB": (128, "float32"),
+    "XGB": (1024, "bfloat16"), "EXA": (128, "float32"), "EXB": (128, "float32"),
     "BXA": (128, "float32"), "BXB": (128, "float32"), "EQA": (128, "bfloat16"), "EQB": (128, "bfloat16"), "PMA": (128, "float32"),
     "PMB": (128, "float32"), "FEA": (128, "float32"), "FEB": (128, "float32"), "MXA": (128, "float32"), "MXB": (128, "float32"),
     "SXA": (8, "int32"), "SXB": (8, "int32"), "HI": (112, "int32"), "LG": (240, "float32"), "LO": (12, "bfloat16"),
@@ -35,6 +36,7 @@ _sb = {
     "ZD1": (32, "float32"), "ZD2": (32, "float32"), "W1": (32, "float32"), "W2": (32, "float32"), "W3": (32, "float32"), "GEM": (64, "float32"),
     "D16": (16, "float32"), "T64": (64, "float32"), "T32": (32, "float32"), "T16": (16, "float32"), "E16": (16, "float32"), "VAL": (48, "float32"),
     "GO2": (24, "float32"), "SV2": (24, "float32"), "JK2": (24, "float32"), "L24": (24, "float32"), "M24": (24, "float32"), "NSL": (12, "float32"),
+    "LQ4": (2048, "bfloat16"), "IDN4": (128, "bfloat16"), "WWA": (128, "float32"), "WWB": (128, "float32"),
     "EBT": (1056, "bfloat16"), "NBO": (128, "bfloat16"), "LM": (192, "bfloat16"), "SHA": (128, "float32"), "SHB": (128, "float32"), "HV": (192, "float32"), "MI": (192, "int32"), "MJ": (192, "int32"), "CC": (64, "float32"), "RT": (16, "float32"), "RLU": (16, "uint16"),
 }
 _apart = ("GC", "FC", "WT", "REP", "LQ", "LQQ", "LW")
@@ -248,16 +250,18 @@ def rank_program(g, core, T, topo):
         k = banks[r % 4]
         mm(b(k, 0, 320), b("REP", 128 * r, 128 * r + 128, p=88), b("GB", p=88), True, True)
         act(b("GNR", 320 * r, 320 * r + 320), b(k, 0, 320), F.Copy)
-    fbank = ["M0", "M1", "SUB0", "SUB1", "M0", "M1", "KEYA", "KEYB", "SUB0", "SUB1", "M1"]
-    for r in range(11):
+    fbank = ["M1", "SUB0", "SUB1", "KEYA", "KEYB", "M1", "SUB0", "SUB1", "KEYA", "KEYB", "SUB0"]
+    def fathers(r):
         k = fbank[r]
         rep = b("REP", 128 * r, 128 * r + 128, p=88)
         mm(b(k, 0, 320), rep, b("FB", 0, 320, p=88), True, False)
         mm(b(k, 0, 320), rep, b("FB", 320, 640, p=88), False, True)
         if r < 6: act(b("F1", 320 * r, 320 * r + 320), b(k, 0, 320), F.Copy)
+        else: cp(b("F1", 320 * r, 320 * r + 320), b(k, 0, 320))
+    for r in range(6): fathers(r)
 
     def more_fathers():
-        for r in range(6, 11): cp(b("F1", 320 * r, 320 * r + 320), b(fbank[r], 0, 320))
+        for r in range(6, 11): fathers(r)
         dma("y", b("F2", 0, M), b("F1", 0, M), "cp0")
     ts(b("PQ", 0, 1), b("PI"), 15, A.bitwise_and)
     ts(b("PQ", 1, 2), b("PI"), 16, A.bitwise_and)
@@ -281,8 +285,10 @@ def rank_program(g, core, T, topo):
     for q in range(16):
         mm(b("M0", 0, 220), lq(q), b("GLR", q, M, 16), q == 0, False)
     for k in range(4):
-        cp(b("SN", 880 * k, 880 * k + 880), b("SI", 880 * k, 880 * k + 880))
-        act(b("NE", 880 * k, 880 * k + 880), b("SN", 880 * k, 880 * k + 880), F.Sign, bias=3520.0, scale=-1.0)
+        c = (880 * k, 880 * k + 880)
+        if k == 3: ts(b("NE", *c), b("SI", *c), M, A.not_equal)
+        cp(b("SN", *c), b("SI", *c))
+        if k < 3: act(b("NE", *c), b("SN", *c), F.Sign, bias=3520.0, scale=-1.0)
     for q in range(16):
         mm(b("M0", 0, 220), lq(q), b("NE", q, M, 16), False, q == 15)
     ts(b("TM"), b("TMP"), -1.0, A.mult)
@@ -292,13 +298,14 @@ def rank_program(g, core, T, topo):
     ts(b("JK"), b("IM"), QC, A.add)
     ts(b("JS"), b("JK"), -3472.0, A.add)
     ts(b("BJ"), b("JK"), -3663.5, A.add)
-    ts(b("LQQ"), b("LQ"), Q16, A.mult)
     ts(b("IP"), b("IP"), 15, A.bitwise_and)
     ts(b("MASK"), b("IP"), 0, A.is_equal)
     ts(b("RES"), b("L15"), 0, A.not_equal)
-    more_fathers()
     def late_constants():
-        ts(b("RESB"), b("RES"), -1e7, A.mult, 1e7, A.add)
+        ts(b("LQQ"), b("LQ"), Q16, A.mult)
+        more_fathers()
+        ts(b("RESB"), b("RES"), -1e12, A.mult, 1e12, A.add)
+        ts(b("IDN4"), b("IDN"), 4096.0, A.mult)
         ts(b("NEGI"), b("IDN"), -1.0, A.mult)
         ts(b("NTHI"), b("IDN"), -524288.0, A.mult)
         ts(b("BIGI"), b("IDN"), 4194304.0, A.mult)
@@ -309,7 +316,6 @@ def rank_program(g, core, T, topo):
 
     def later_constants():
         ts(W16, b("WT"), 0.0625, A.mult)
-        ts(b("LW"), b("LQ"), W16, A.mult)
         ts(b("NBO"), b("BO"), -1.0, A.mult)
         for j in (0, 12): cp(b("JK2", j, j + 12), b("JK"))
         ts(QP, b("PQ", 0, 1), 1.0, A.add)
@@ -339,7 +345,7 @@ def rank_program(g, core, T, topo):
 
     def lanes(t, meanwhile):
         r = 107 * t % NB
-        sign = 10
+        sign = SIGN[1 if t else 0]
         if t == 0:
             ts(b("OKR", 0, 220), b("M0", 0, 220), 0, A.is_equal)
             ts(b("NOK", 0, 220), b("M0", 0, 220), 0, A.not_equal)
@@ -361,8 +367,9 @@ def rank_program(g, core, T, topo):
             act(b("XLR", 0, 512), ind(LX, b("ARO", 0, 32), hi=64), F.Copy)
             act(b("XLR", 3584, 4096), ind(LX, b("ARO", 32, 64), hi=64), F.Copy)
         meanwhile()
+        ts(b("KO", 0, sign), b("KA", 0, sign), 0.5, A.mult, NB / 2.0, A.add)
+        if sign < 12: cp(b("KO", sign, 12), b("KA", sign, 12))
         ts(b("KA", 0, sign), b("KA", 0, sign), 0.5, A.mult, NB / 2.0, A.add)
-        cp(b("KO"), b("KA"))
         tt(b("OH"), ind("PL", b("KO"), hi=240), b("JREP"), A.is_equal)
         for q in range(16):
             mm(b("M0", 0, 12), lq(q, "LQQ"), b("OH", q, 192, 16), q == 0, q == 15)
@@ -391,26 +398,29 @@ def rank_program(g, core, T, topo):
     def starts(t):
         F_ = "F2" if t % 2 else "F1"
         cp(b("HRU"), ind("IOTA", b("HU")))
-        act(b("XLR", 1280, 2048), ind("X", b("HRU", 48, 96)), F.Copy)
+        act(b("XLR", 1024, 2048), ind("X", b("HRU", 32, 96)), F.Copy)
         tt(b("G1"), ind(F_, b("HU")), b("MASK", 0, 192), A.mult)
         scan(b("G2"), b("RES", 0, 192), b("G1"), 0.0, A.mult, A.add)
         cp(b("CU", 2, 14), b("G2", 15, 192, 16))
-        cp(b("P0"), b("G2", 15, 192, 16))
+
+    def arrivals(t):
         if t:
             if t == 1: fill(b("EQA", 0, 32), 0.0)
             LX = "LX%d" % t
             for q in range(16):
                 mm(b("M1", 0, 4), lq(q, "LW"), b(LX, q, 64, 16), q == 0, q == 15)
+            yield
             cp(b("HI", 0, 4), b("M1", 0, 4))
+            yield
             ts(b("HI", 0, 4), b("HI", 0, 4), 63, A.bitwise_and)
+            yield
             cp(b("CU", 0, 2), b("HI", 0, 2))
             cp(b("CU", 14, 16), b("HI", 2, 4))
 
-    def starts_a(t):
-        cp(b("XLR", 512, 1280), ind("X", b("HRU", 0, 48)))
-
     def starts_b(t):
         act(b("XLR", 2048, 3584), ind("X", b("HRU", 96, 192)), F.Copy)
+
+    def sg_at(z, lo, hi): return b("KEY" + z, 256 + lo, 256 + hi)
 
     def hist(e, lo, hi): return b("HI", 16 * e + lo, 16 * e + hi)
 
@@ -432,29 +442,27 @@ def rank_program(g, core, T, topo):
         sub = ("SUB0", "M0") if z == "A" else ("SUB1", "M1")
         nb = kc // 2
         cp(b(su, 0, n), ind("SN", cu))
-        ts(d3(sg, 0, nb), b(su, 0, n), I4, A.add)
+        ts(d3(sg, 0, nb), b(su, 0, n), I4 if e <= 3 else 1.0, A.add)
         if between: between()
         for P in (0, 1):
             mm(d3(pw, 0, nb, 16 * P, 16 * P + 16), b("QD%d" % P), d3(sg, 0, nb, 16 * P, 16 * P + 16), True, False)
             mm(d3(pw, 0, nb, 16 * P, 16 * P + 16), b("QO%d" % P), d3(sg, 0, nb, 16 - 16 * P, 32 - 16 * P), False, True)
+        flush()
         act(b(xg, 0, 256 * ks), ind("X", b(su, 16 * kv, n)), F.Copy)
         if behind: behind()
         x0 = 256 * k0
         c4 = min(kv, 4)
-        for lo, hi in [(0, c4)] + ([(4, kv)] if kv > 4 else []):
-            tt(b(df, 256 * lo, 256 * hi), ind("X", b(su, 16 * lo, 16 * hi)), b("XLR", x0 + 256 * lo, x0 + 256 * hi), A.subtract)
-            yield
+        tt(b(df, 0, 256 * kv), ind("X", b(su, 0, 16 * kv)), b("XLR", x0, x0 + 256 * kv), A.subtract)
+        yield
         subs = [(kv + 2 * j, min(kv + 2 * j + 2, kc), sub[j]) for j in range((ks + 1) // 2)]
         for lo, hi, bank in subs:
             w = 256 * (hi - lo)
             mm(b(bank, 0, w), b("IDN"), b(xg, 256 * (lo - kv), 256 * (hi - kv)), True, False)
             mm(b(bank, 0, w), b("NEGI"), b("XLR", x0 + 256 * lo, x0 + 256 * hi), False, True)
-        act(d3(dd, 0, c4), b(df, 0, 256 * c4), F.Abs)
+        act(d3(dd, 0, kv), b(df, 0, 256 * kv), F.Abs)
         for lo, hi, bank in subs:
             act(d3(dd, lo, hi), b(bank, 0, 256 * (hi - lo)), F.Abs)
-        if kv > 4:
-            act(d3(dd, 4, kv), b(df, 1024, 256 * kv), F.Abs)
-        sig = b("SIG" + z, 0, n)
+        sig = sg_at(z, 0, n)
         if e <= 3:
             i0, i1 = o0 - k0, o1 - k0
             m0, m1 = o0 - 2, o1 - 2
@@ -477,32 +485,56 @@ def rank_program(g, core, T, topo):
             yield
             scan(b("BX" + z, 16 * i0, 16 * i1), b("RES", 0, 16 * L), b("EX" + z, 16 * i0, 16 * i1), 0.0, A.mult, A.add)
             yield
+        else:
+            yield
         call("v", V.transpose, sig, [d3(pw, 0, nb)], [], {})
         yield
         if e <= 3:
-            tt(b("EQ" + z, 16 * i0, 16 * i1), b("SIG" + z, 16 * i0, 16 * i1), b("BX" + z, 16 * i0, 16 * i1), A.is_equal)
+            tt(b("EQ" + z, 16 * i0, 16 * i1), sg_at(z, 16 * i0, 16 * i1), b("BX" + z, 16 * i0, 16 * i1), A.is_equal)
             yield
-        for lo, hi in ((0, c4), (c4, kc)):
-            o = b(key, 16 * lo, 16 * hi)
-            mm(o, b("IDN"), b("SLOT", 16 * lo, 16 * hi), True, False)
-            if e <= 3:
-                mm(o, b("NTHI"), b("ONES", 16 * lo, 16 * hi), False, False)
-            for q in range(16):
-                mm(o, lq(q), d3(dd, lo, hi, 16 * q, 16 * q + 16), False, q == 15 and e > 3)
-            if e <= 3:
-                mm(o, b("BIGI"), b("EQ" + z, 16 * lo, 16 * hi), False, True)
+        def keys():
+            for lo, hi in ((0, c4), (c4, kc)):
+                o = b(key, 16 * lo, 16 * hi)
+                mm(o, b("IDN" if e <= 3 else "IDN4"), b("SLOT", 16 * lo, 16 * hi), True, False)
+                if e <= 3:
+                    mm(o, b("NTHI"), b("ONES", 16 * lo, 16 * hi), False, False)
+                for q in range(16):
+                    mm(o, lq(q, "LQ" if e <= 3 else "LQ4"), d3(dd, lo, hi, 16 * q, 16 * q + 16), False, q == 15 and e > 3)
+                if e <= 3:
+                    mm(o, b("BIGI"), b("EQ" + z, 16 * lo, 16 * hi), False, True)
+        if t and e == 1 and z == "A":
+            pending.append(keys)
+        else:
+            keys()
+
+    pending = []
+    def flush():
+        while pending: pending.pop()()
 
     def back(t, e, z):
         k0, k1, o0, o1 = rng(t, z)
         kc = k1 - k0
         n = 16 * kc
         key, pm, fe, mx, sx = b("KEY" + z, 0, n), b("PM" + z, 0, n), b("FE" + z, 0, n), b("MX" + z, 0, n), b("SX" + z, 0, kc)
-        if e <= 3: scan(pm, b("RES", 0, n), key, 0.0, A.mult, A.min)
-        else: scan(pm, b("RESB", 0, n), key, 1e7, A.add, A.min)
+        if e > 3:
+            ww = b("WW" + z, 0, n)
+            scan(pm, b("RESB", 0, n), key, 1e12, A.add, A.min)
+            yield
+            tt(fe, key, pm, A.subtract)
+            yield
+            tt(ww, sg_at(z, 0, n), fe, A.subtract)
+            yield
+            scan(mx, fe, ww, 0.0, A.min, A.max)
+            yield
+            if e < 6:
+                ts(b("CU", k0, k1), b("MX" + z, 15, n, 16), -1.0, A.add)
+            ts(hist(e, k0, k1), b("MX" + z, 15, n, 16), -1.0, A.add)
+            return
+        scan(pm, b("RES", 0, n), key, 0.0, A.mult, A.min)
         yield
         tt(fe, key, pm, A.is_equal)
         yield
-        tt(fe, fe, b("SIG" + z, 0, n), A.mult)
+        tt(fe, sg_at(z, 0, n), fe, A.mult)
         yield
         f0 = b("FE" + z, 0, n, 16)
         if e <= 2: tt(f0, f0, b(UP[e], k0, k1), A.max)
@@ -635,19 +667,20 @@ def rank_program(g, core, T, topo):
         yield
         cp(b("YREP"), ind("IOTA", b("LU", 0, 12)))
         yield
-        scan(b("SX"), b("RES", 0, 192), b("EZS"), 0.0, A.mult, A.add)
+        yx, sx = b("M0", 0, 192), b("M0", 192, 384)
+        scan(sx, b("RES", 0, 192), b("EZS"), 0.0, A.mult, A.add)
         yield
         ts(b("EZY", 0, 192, 16), YL, 20000.0, A.add)
         yield
         tt(b("MI"), ind("X", b("LU", 12, 24)), b("XLR", 512, 3584, 16), A.add)
         yield
-        scan(b("YX"), b("RES", 0, 192), b("EZY"), 0.0, A.mult, A.add)
+        scan(yx, b("RES", 0, 192), b("EZY"), 0.0, A.mult, A.add)
         yield
         for k in range(11):
             ts(b("EBY", off[k], off[k + 1]), b("YREP", 16 * k + 16, 192), c1("LG", 12 * YLs + k), A.is_equal)
             yield
-        tt(b("DGY"), b("YREP"), b("YX"), A.is_equal)
-        tt(b("DGS"), b("SREP"), b("SX"), A.is_equal)
+        tt(b("DGY"), b("YREP"), yx, A.is_equal)
+        tt(b("DGS"), b("SREP"), sx, A.is_equal)
         mm(b("M1", 0, 192), b("BO"), b("LM"), True, False)
         mm(b("M1", 0, 192), b("BO"), b("DGY"), False, False)
         for k in range(11):
@@ -662,10 +695,10 @@ def rank_program(g, core, T, topo):
         if not last:
             tt(b("EA"), b("SY"), b("SREP"), A.is_equal)
             mm(b("SUB0", 0, 192), b("TRI2"), b("EA"), True, True)
-            act(b("DS"), b("SREP"), F.Copy, bias=3520.0, scale=-1.0)
+            act(b("KEYB", 0, 192), b("SREP"), F.Copy, bias=3520.0, scale=-1.0)
         jk = b("JK")
         tt(b("VAL", 0, 12), SL, jk, A.subtract)
-        tt(b("VAL", 12, 24), b("H"), jk, A.subtract)
+        if not last: tt(b("VAL", 12, 24), b("H"), jk, A.subtract)
         tt(b("VAL", 24, 36), YL, jk, A.subtract)
         tt(b("VAL", 36, 48), SL, jk, A.subtract)
         ts(b("MJ"), b("MI"), 1, A.arith_shift_right)
@@ -687,22 +720,32 @@ def rank_program(g, core, T, topo):
         last = t == 2
         cp(ind("X", b("LU", 24, 36)), b("MJ"))
         if last: dma("y", T.xo[:, 0:M], b("X", 0, M), "st0")
+        cp(ind("F2", b("LU", 24, 36)), b("HREP"))
+
+    def write_first(t):
         ts(b("M24", 0, 12), b("SUB1", 0, 12), 24, A.is_gt)
         for j in (0, 12): tt(b("SV2", j, j + 12), b("M24", 0, 12), b("GO2", 0, 12), A.mult)
-        cp(ind("F2", b("LU", 24, 36)), b("HREP"))
         targets(48, "SV2", 24)
         cp(ind("F1", b("LU", 60, 72)), b("HREP"))
 
     def write_sons(t):
         ts(b("HV"), b("SREP"), E0, A.mult, C0, A.add)
-        cp(ind("SN", b("LU", 36, 48)), b("HV"))
+        yield
         ts(b("FF"), b("SUB0", 0, 192), -1, A.is_equal)
-        tt(b("FF"), b("FF"), b("DS"), A.mult)
-        tt(b("NC"), b("FF"), b("SY"), A.add)
+        yield
+        cp(ind("SN", b("LU", 36, 48)), b("HV"))
+        yield
+        tt(b("KEYB", 192, 384), b("FF"), b("KEYB", 0, 192), A.mult)
+        yield
+        tt(b("NC"), b("KEYB", 192, 384), b("SY"), A.add)
+        yield
         cp(ind("SN", b("LU", 48, 60)), b("NC"))
+        yield
         if t == 1:
             ts(b("CC"), ind("SN", b("RLU", 4, 8)), N1c, A.mult)
+            yield
             tt(b("CC"), b("CC"), b("NEWT"), A.add)
+            yield
             cp(ind("SN", b("RLU", 4, 8)), b("CC"))
 
     def get_back(t):
@@ -719,19 +762,21 @@ def rank_program(g, core, T, topo):
 
     def new_men(t):
         rl, nc = "RL%d" % t, 3536 + 64 * (t - 1)
-        cp(b("X", nc, nc + 64), b(rl, 0, 64))
         tt(b("RT", 0, 4), b("SENT", 4 * (t - 1), 4 * t), b(rl, 64, 68), A.mult)
+        yield
         cp(b("RLU", 0, 4), b("RT", 0, 4))
+        yield
+        cp(b("X", nc, nc + 64), b(rl, 0, 64))
+        yield
         cp(b("F1", nc, nc + 64), ind("IOTA", b("RLU", 0, 4)))
+        yield
         cp(b("F2", nc, nc + 64), b("F1", nc, nc + 64))
 
     def rest(t):
-        write_sons(t)
-        if t: new_men(t)
+        weave(write_sons(t), new_men(t) if t else [], arrivals(t + 1))
 
     for t in range(3):
         lanes(t, (lambda: rest(t - 1)) if t else late_constants)
-        ts(lg(REAL), b("H"), 3520, A.not_equal)
         starts(t)
         F_ = "F2" if t % 2 else "F1"
         q1, q2 = b("UP1", 2, 14), b("Q2")
@@ -742,28 +787,38 @@ def rank_program(g, core, T, topo):
             yield from climb(F_, q1, q2)
             tt(lg(DQ), q2, q1, A.subtract)
             tt(lg(DP), q1, b("P0"), A.subtract)
-        weave(front(t, 1, "A", lambda: starts_a(t), lambda: starts_b(t)))
+        def at_once():
+            cp(b("P0"), b("G2", 15, 192, 16))
+            cp(b("XLR", 512, 1024), ind("X", b("HRU", 0, 32)))
+        weave(front(t, 1, "A", at_once, lambda: starts_b(t)))
+        if t < 2: ts(lg(REAL), b("H"), 3520, A.not_equal)
         weave(front(t, 1, "B", None if t else later_constants), climbs())
         act(b("HREP"), ind("IOTA", b("HU")), F.Copy)
         weave(back(t, 1, "A"))
         for e in range(2, 7):
             weave(front(t, e, "A"), back(t, e - 1, "B"))
             weave(front(t, e, "B"), back(t, e, "A"))
-        weave(back(t, 6, "B"), partial(t))
+            if t == 0 and e < 4:
+                for j in (0, 1024) if e == 2 else ():
+                    act(b("LQ4", j, j + 1024), b("LQ", j, j + 1024), F.Copy, scale=4096.0)
+                for j in (0, 1024) if e == 3 else ():
+                    act(b("LW", j, j + 1024), b("LQ", j, j + 1024), F.Copy, scale=W16)
+        flush()
+        weave(partial(t))
+        weave(back(t, 6, "B"))
         weave(give_back(t) if t else [], own_found())
         weave(adopt(t), send(t) if t < 2 else [])
         if t < 2:
             if t: get_back(t)
             recount()
         write_men(t)
+        write_first(t)
         if t == 2:
-            fill(b("F1", M, M + 16), 0.0)
-            fill(b("F2", M, M + 16), 0.0)
-            fill(b("X", M, M + 16), 0.0)
+            for k in ("F1", "F2", "X"): num(b(k, M, M + 16), 16, 0)
             dma("s", T.fo[:, 0:M], (T.F1[0:128:16, 0:M], [("F1", 0, M)]), "st1")
             dma("y", T.f2o[:, 0:M], (T.F2[0:128:16, 0:M], [("F2", 0, M)]), "st2")
             get_back(t)
-            new_men(t)
+            weave(new_men(t))
     dma("y", T.xo[:, M:W], b("X", M, W), "st3")
     dma("s", T.fo[:, M:W], (T.F1[0:128:16, M:W], [("F1", M, W)]), "st4")
     dma("y", T.f2o[:, M:W], (T.F2[0:128:16, M:W], [("F2", M, W)]), "st5")

from concourse.mybir import dt, AluOpType as A, AxisListType, ActivationFunctionType as F

M, W, WX, EMPTY, EXT = 3520, 3664, 3920, 3520, 3856
NB = 229
SIGN = [10, 10]
KS = [[3, 3, 3, 2, 2, 2], [4, 4, 4, 4, 4, 4]]

_sb = {
    "SI": (3520, "int32"), "SN": (WX, "float32"), "X": (WX, "bfloat16"), "F1": (WX, "float32"), "F2": (WX, "float32"),
    "GNR": (W, "bfloat16"), "GLR": (M, "bfloat16"), "NE": (M, "bfloat16"), "IOTA": (WX, "float32"), "ADD": (WX, "bfloat16"),
    "GC": (320, "int32"), "FC": (320, "int32"), "FI": (640, "int32"), "FB": (640, "bfloat16"), "GB": (320, "bfloat16"),
    "WT": (1, "bfloat16"), "I1": (256, "int32"), "PI": (1, "int32"), "PQ": (4, "int32"), "IP": (256, "int32"), "L15": (256, "int32"),
    "IM": (12, "int32"), "COL": (16, "float32"), "MASK": (256, "float32"), "RES": (256, "float32"), "RESB": (256, "float32"),
    "SLOT": (256, "bfloat16"), "LOWM": (192, "float32"), "JREP": (192, "float32"), "JK": (12, "float32"), "JS": (12, "float32"),
    "BJ": (12, "float32"), "ARO": (64, "uint16"), "ONES": (1408, "bfloat16"), "REP": (1408, "bfloat16"), "BO": (128, "bfloat16"),
    "BT": (128, "bfloat16"), "BO8": (8, "bfloat16"), "TMP": (128, "bfloat16"), "TM": (128, "bfloat16"), "TMX": (128, "bfloat16"),
    "TRI": (128, "bfloat16"), "TRI2": (128, "bfloat16"), "IDN": (128, "bfloat16"), "NEGI": (128, "bfloat16"), "BIGI": (128, "bfloat16"),
    "I255": (128, "bfloat16"), "SHU": (128, "bfloat16"), "SHD": (128, "bfloat16"),
    "QD0": (128, "float32"), "QO0": (128, "float32"), "QD1": (128, "float32"), "QO1": (128, "float32"),
    "LQ": (2048, "bfloat16"), "LQQ": (2048, "bfloat16"), "LW": (2048, "bfloat16"), "ONEF": (256, "float32"), "NEWT": (64, "float32"),
    "NOK": (240, "bfloat16"), "OKR": (240, "bfloat16"), "SB": (240, "float32"), "PL": (240, "float32"), "CM0": (240, "float32"),
    "CM1": (240, "float32"), "SJ": (240, "float32"), "KA": (12, "float32"), "KO": (12, "uint16"), "OH": (192, "bfloat16"),
    "HB": (12, "float32"), "HT": (12, "float32"), "HE": (12, "float32"), "H": (12, "float32"), "HU": (12, "uint16"), "HREP": (192, "float32"),
    "HRU": (192, "uint16"), "XLR": (4096, "bfloat16"), "G1": (192, "float32"), "G2": (192, "float32"), "P0": (12, "float32"),
    "P0P": (12, "float32"), "Q1": (12, "float32"), "Q2": (12, "float32"), "PX": (12, "float32"), "PU": (12, "uint16"), "CU": (16, "uint16"),
    "SUA": (128, "uint16"), "SUB": (128, "uint16"), "DFA": (2048, "bfloat16"), "DFB": (2048, "bfloat16"), "XGA": (1024, "bfloat16"),
    "XGB": (1024, "bfloat16"), "EXA": (128, "float32"), "EXB": (128, "float32"),
    "BXA": (128, "float32"), "BXB": (128, "float32"), "EQA": (128, "bfloat16"), "EQB": (128, "bfloat16"), "PMA": (128, "float32"),
    "PMB": (128, "float32"), "FEA": (128, "float32"), "FEB": (128, "float32"), "MXA": (128, "float32"), "MXB": (128, "float32"),
    "SXA": (8, "int32"), "SXB": (8, "int32"), "HI": (112, "int32"), "LG": (240, "float32"), "LO": (12, "bfloat16"),
    "SLU": (12, "uint16"), "SR0": (384, "float32"), "SR1": (384, "float32"), "NTHI": (128, "bfloat16"), "UP1": (16, "float32"), "UP2": (16, "float32"), "G4": (64, "float32"), "G5": (64, "float32"), "SENT": (8, "float32"), "S4U": (4, "uint16"),
    "GE": (16, "float32"), "AL": (32, "float32"), "RU": (4, "uint16"), "LU": (96, "uint16"), "YREP": (192, "float32"), "SREP": (192, "float32"),
    "EZY": (192, "float32"), "EZS": (192, "float32"), "YX": (192, "float32"), "SX": (192, "float32"), "YM": (192, "float32"), "SM": (192, "float32"),
    "DGY": (192, "bfloat16"), "DGS": (192, "bfloat16"), "EBY": (1056, "bfloat16"), "EBS": (1056, "bfloat16"), "SY": (192, "float32"),
    "NY": (192, "bfloat16"), "EA": (192, "bfloat16"), "FF": (192, "float32"), "DS": (192, "float32"), "NC": (192, "float32"),
    "ZD1": (32, "float32"), "ZD2": (32, "float32"), "W1": (32, "float32"), "W2": (32, "float32"), "W3": (32, "float32"), "GEM": (64, "float32"),
    "D16": (16, "float32"), "T64": (64, "float32"), "T32": (32, "float32"), "T16": (16, "float32"), "E16": (16, "float32"), "VAL": (48, "float32"),
    "GO2": (24, "float32"), "SV2": (24, "float32"), "JK2": (24, "float32"), "L24": (24, "float32"), "M24": (24, "float32"), "NSL": (12, "float32"),
    "LQ4": (2048, "bfloat16"), "IDN4": (128, "bfloat16"), "WWA": (128, "float32"), "WWB": (128, "float32"),
    "EBT": (1056, "bfloat16"), "NBO": (128, "bfloat16"), "LM": (192, "bfloat16"), "SHA": (128, "float32"), "SHB": (128, "float32"), "HV": (192, "float32"), "MI": (192, "int32"), "MJ": (192, "int32"), "CC": (64, "float32"), "RT": (16, "float32"), "RLU": (16, "uint16"),
}
_apart = ("GC", "FC", "WT", "REP", "LQ", "LQQ", "LW")
AT, _used = {}, {}
for _k, (_n, _d) in _sb.items():
    if _n <= 1056 and _k not in _apart:
        AT[_k] = ("all_" + _d, _used.get(_d, 0), _n)
        _used[_d] = _used.get(_d, 0) + (_n + 15) // 16 * 16
    else:
        AT[_k] = (_k, 0, _n)
SCRATCH = {k: ("sbuf", [128, n], d) for k, (n, d) in _sb.items() if AT[k][0] == k}
for _d, _n in _used.items(): SCRATCH["all_" + _d] = ("sbuf", [128, _n], _d)
for _n in ("D3A", "D3B"): SCRATCH[_n] = ("sbuf", [128, 8, 256], "bfloat16")
for _n in ("SGA", "SGB"): SCRATCH[_n] = ("sbuf", [128, 4, 32], "float32")
for _n in ("PY0", "PY1", "LX1", "LX2"): SCRATCH[_n] = ("sbuf", [128, 80], "bfloat16")
for _n in ("RS1", "RS2", "RL1", "RL2"): SCRATCH[_n] = ("sbuf", [128, 72], "bfloat16")
for _n in ("KEYA", "KEYB", "SUB0", "SUB1", "M0", "M1"): SCRATCH[_n] = ("psum", [128, 512], "float32")
for _n in ("PWA", "PWB"): SCRATCH[_n] = ("psum", [128, 16, 32], "float32")
PSUM = {k for k, v in SCRATCH.items() if v[0] == "psum"}
SEMAPHORES = (["e_v", "e_s", "e_t", "e_g"] + ["ld%d" % i for i in range(12)] + ["st%d" % i for i in range(8)] + ["cp0"]
              + ["snd_out%d" % i for i in (0, 1)] + ["snd_in%d" % i for i in (0, 1)] + ["ret_out%d" % i for i in (1, 2)] + ["ret_in%d" % i for i in (1, 2)])


def rank_program(g, core, T, topo):
    rank = T.rank_of(core)
    if rank is None:
        return
    N = len(T.cores)
    queue = {"v": g.vector, "s": g.scalar, "t": g.tensor, "g": g, "y": g.sync}
    know = {q: {} for q in queue}
    count = {}
    clocks = {}
    log = {}

    def need(q, acc, write, deps):
        name, lo, hi = acc
        ps = name in PSUM
        for l, h, w, q2, tok in log.get(name, ()):
            if not ps and (h <= lo or hi <= l):
                continue
            if q2 == q and (q == "t" or not (w or write)):
                continue
            if w or write or (ps and q2 != q):
                deps.add(tok)

    def book(q, acc, write, tok):
        name, lo, hi = acc
        if name in PSUM:
            lo, hi = 0, 1 << 20
        old = log.setdefault(name, [])
        if write or name in PSUM:
            old[:] = [e for e in old if not (e[0] >= lo and e[1] <= hi)]
        old.append((lo, hi, write, q, tok))

    def waits(q, deps):
        for tok in sorted(deps, key=lambda t: -t[1]):
            sem, val = tok
            if know[q].get(sem, 0) >= val:
                continue
            queue[q].wait_ge(T.sem[sem], val)
            know[q][sem] = val
            for s2, v2 in clocks[tok].items():
                if know[q].get(s2, 0) < v2:
                    know[q][s2] = v2

    def call(q, fn, out, ins, extra, kw, sem=None, step=1):
        reads = [a for o in ins if isinstance(o, tuple) for a in o[1]]
        writes = list(out[1][:1])
        reads += out[1][1:]
        k2 = {}
        for k, v in kw.items():
            if isinstance(v, tuple):
                (writes if k == "accum_out" else reads).extend(v[1])
                k2[k] = v[0]
            else:
                k2[k] = v
        deps = set()
        for a in reads: need(q, a, False, deps)
        for a in writes: need(q, a, True, deps)
        waits(q, deps)
        ins_ = fn(out[0], *[o[0] if isinstance(o, tuple) else o for o in ins], *extra, **k2)
        sem = sem or "e_" + q
        count[sem] = count.get(sem, 0) + step
        ins_.then_inc(T.sem[sem], step)
        tok = (sem, count[sem])
        clocks[tok] = dict(know[q])
        for a in reads: book(q, a, False, tok)
        for a in writes: book(q, a, True, tok)

    def b(name, lo=0, hi=None, st=1, p=None):
        name, off, n = AT[name] if name in AT else (name, 0, SCRATCH[name][1][1])
        lo, hi = lo + off, (n if hi is None else hi) + off
        ap = T[name][:, lo:hi:st] if p is None else T[name][0:p, lo:hi:st]
        return (ap, [(name, lo, hi)])

    def c1(name, j): return b(name, j, j + 1)

    def d3(name, lo, hi, a=None, z=None):
        n = SCRATCH[name][1][2]
        ap = T[name][:, lo:hi, :] if a is None else T[name][:, lo:hi, a:z]
        return (ap, [(name, lo * n, hi * n)])

    def ind(win, off, lo=0, hi=None):
        w = b(win, 0, WX if hi is None else hi)
        return (w[0].indirect(off[0]), w[1] + off[1])

    V = g.vector
    def tt(out, x, y, op): call("v", V.tensor_tensor, out, [x, y], [op], {})
    def ts(out, x, s1, op, s2=None, op2=None):
        if op2 is None: call("v", V.tensor_scalar, out, [x, s1], [None, op], {})
        else: call("v", V.tensor_scalar, out, [x, s1, s2], [op, op2], {})
    def cp(out, x): call("v", V.tensor_copy, out, [x], [], {})
    def fill(out, c): call("v", V.memset, out, [], [c], {})
    def scan(out, x, y, init, o0, o1): call("v", V.tensor_tensor_scan, out, [x, y], [init, o0, o1], {})
    def act(out, x, f, **kw): call("s", g.scalar.activation, out, [x], [f], kw)
    def mm(out, l, r, start, stop): call("t", g.tensor.matmul, out, [l, r], [start, stop], {})
    def gop(fn, out, ins, extra, **kw): call("g", fn, out, ins, extra, kw)
    def dma(q, out, x, sem):
        o = out if isinstance(out, tuple) else (out, [])
        deps = set()
        rd = x[1] if isinstance(x, tuple) else []
        for a in rd: need(q, a, False, deps)
        for a in o[1]: need(q, a, True, deps)
        waits(q, deps)
        count[sem] = count.get(sem, 0) + 16
        queue[q].dma_start(o[0], x[0] if isinstance(x, tuple) else x).then_inc(T.sem[sem], 16)
        tok = (sem, count[sem])
        clocks[tok] = dict(know[q])
        for a in rd: book("dma", a, False, tok)
        for a in o[1]: book("dma", a, True, tok)

    def remote(to, dst, src, rsem, lsem):
        peer = T.cores[to]
        deps = set()
        need("g", (src, 0, 80), False, deps)
        waits("g", deps)
        rid, pid, _ = topo.addr(peer)
        n = len(topo.engines(core, peer))
        g.remote_dma(T[dst][:], T[src][:], T.sem[rsem], T.sem[lsem], pid, rid, topo.mask(core, peer))
        count[lsem] = n
        book("rem", (src, 0, 72), False, (lsem, n))
        clocks[(lsem, n)] = {}

    def arrive(frm, buf, sem):
        n = len(topo.engines(T.cores[frm], core))
        count[sem] = n
        clocks[(sem, n)] = {}
        book("rem", (buf, 0, 80), True, (sem, n))

    dma("y", b("GC", p=88), T.gn[:], "ld0")
    dma("y", b("FC", p=88), T.fa[:], "ld1")
    dma("y", b("WT"), T.w[:], "ld8")
    for k in range(4):
        dma("y" if k % 2 else "s", b("SI", 880 * k, 880 * k + 880), T.sn[:, 880 * k:880 * k + 880], "ld%d" % (2 + k))
    dma("y", b("X", 0, 1760), T.x[:, 0:1760], "ld6")
    dma("s", b("X", 1760, M), T.x[:, 1760:M], "ld7")

    fill(b("ONES"), 1.0)
    ia, af = g.iota, g.affine_select
    def num(out, n, c, step=0):
        gop(ia, out, [], [[[step, n]], c, 0], allow_small_or_imprecise_dtypes=True)
    gop(ia, b("PI"), [], [[[1, 1]], 0, 1])
    gop(af, b("REP"), [b("ONES")], [[[-1, 11], [-11, 8], [0, 16]], A.is_equal, 0.0, 0, 1])
    gop(af, b("BT"), [b("ONES", 0, 128)], [[[-16, 8], [0, 16]], A.is_ge, 0.0, 0, 1])
    gop(af, b("BO"), [b("BT")], [[[16, 8], [0, 16]], A.is_ge, 0.0, 15, -1])
    gop(af, b("IDN"), [b("ONES", 0, 128)], [[[-1, 128]], A.is_equal, 0.0, 0, 1])
    gop(af, b("TMP"), [b("BO")], [[[-1, 128]], A.is_ge, 0.0, 0, 1])
    gop(af, b("TRI"), [b("BO")], [[[1, 128]], A.is_ge, 0.0, -1, -1])
    gop(af, b("SHU"), [b("ONES", 0, 128)], [[[1, 128]], A.is_equal, 0.0, -16, -1])
    gop(af, b("SHD"), [b("ONES", 0, 128)], [[[1, 128]], A.is_equal, 0.0, 16, -1])
    num(b("GNR", M, W), W - M, 0)
    num(b("OKR", 220, 240), 20, 0)
    num(b("NOK", 220, 240), 20, 1)
    num(b("PL", NB, 240), 240 - NB, 5000)
    num(b("JREP"), 192, -255, 1)
    gop(ia, b("IM"), [], [[[16, 12]], W, 0])
    gop(ia, b("I1", 0, 192), [], [[[1, 192]], 0, 0])
    gop(ia, b("IP"), [], [[[1, 256]], 128, -1])
    gop(ia, b("L15"), [], [[[0, 16], [1, 16]], 0, 0])
    gop(ia, b("SLOT"), [], [[[0, 16], [1, 16]], 0, 0], allow_small_or_imprecise_dtypes=True)
    num(b("SN", M, WX), WX - M, 3520)
    num(b("X", M, WX), WX - M, 0)
    num(b("X", M, M + 1), 1, 4096)
    for f in ("F1", "F2"):
        num(b(f, M, EXT), EXT - M, 0)
        num(b(f, M, M + 1), 1, 3520)
        num(b(f, EXT, WX), WX - EXT, 3520)
    num(b("IOTA"), WX, 0, 1)
    for k in "AB":
        num(b("EX" + k), 128, 4096)
        num(b("EQ" + k), 128, 0)
    for k in "12":
        num(b("UP" + k), 16, 3520)
    for k in "12":
        num(b("ZD" + k, 0, 16), 16, 0)
    gop(ia, b("HI"), [], [[[0, 112]], 0, 0])
    for k in "01":
        num(b("SR" + k, 0, 64), 64, 3520)
        num(b("PY" + k, 64, 80), 16, 0)
    for n in ("RS1", "RS2"): num(b(n, 64, 72), 8, 0)
    gop(ia, b("LM"), [], [[[1, 12], [0, 16]], 0, 0], allow_small_or_imprecise_dtypes=True)
    num(b("ADD"), WX, 0)

    cp(b("GB", p=88), b("GC", p=88))
    ts(b("FI", 0, 320, p=88), b("FC", p=88), 6, A.arith_shift_right)
    ts(b("FI", 320, 640, p=88), b("FC", p=88), 63, A.bitwise_and)
    ts(b("FB", 0, 320, p=88), b("FI", 0, 320, p=88), 64.0, A.mult)
    cp(b("FB", 320, 640, p=88), b("FI", 320, 640, p=88))
    banks = ["SUB0", "SUB1", "M0", "M1"]
    for r in range(11):
        k = banks[r % 4]
        mm(b(k, 0, 320), b("REP", 128 * r, 128 * r + 128, p=88), b("GB", p=88), True, True)
        act(b("GNR", 320 * r, 320 * r + 320), b(k, 0, 320), F.Copy)
    fbank = ["M1", "SUB0", "SUB1", "KEYA", "KEYB", "M1", "SUB0", "SUB1", "KEYA", "KEYB", "SUB0"]
    def fathers(r):
        k = fbank[r]
        rep = b("REP", 128 * r, 128 * r + 128, p=88)
        mm(b(k, 0, 320), rep, b("FB", 0, 320, p=88), True, False)
        mm(b(k, 0, 320), rep, b("FB", 320, 640, p=88), False, True)
        if r < 6: act(b("F1", 320 * r, 320 * r + 320), b(k, 0, 320), F.Copy)
        else: cp(b("F1", 320 * r, 320 * r + 320), b(k, 0, 320))
    for r in range(6): fathers(r)

    def more_fathers():
        for r in range(6, 11): fathers(r)
        dma("y", b("F2", 0, M), b("F1", 0, M), "cp0")
    ts(b("PQ", 0, 1), b("PI"), 15, A.bitwise_and)
    ts(b("PQ", 1, 2), b("PI"), 16, A.bitwise_and)
    QC, I4, E0, C0, N1c, E1c, H0, H1, Q16, W16, QP = [c1("COL", j) for j in range(11)]
    cp(QC, b("PQ", 0, 1))
    ts(I4, b("PQ", 0, 1), 4096.0, A.mult, 4096.0, A.add)
    ts(E0, b("PQ", 0, 1), 0, A.is_equal)
    ts(C0, E0, -3520.0, A.mult, 3520.0, A.add)
    ts(N1c, b("PQ", 0, 1), 1, A.not_equal)
    ts(E1c, b("PQ", 0, 1), 1, A.is_equal)
    ts(H0, b("PQ", 1, 2), 0, A.is_equal)
    ts(H1, b("PQ", 1, 2), 0, A.not_equal)
    ts(Q16, b("PQ", 0, 1), 0.0625, A.mult)
    ts(b("BO8"), b("BO", 0, 128, 16), 16.0, A.mult)
    fill(b("LQ"), 0.0)
    for q in range(16):
        cp((T.LQ[:, q * 128 + q:q * 128 + 128:16], [("LQ", q * 128, q * 128 + 128)]), b("BO8"))
    ts(b("GLR"), b("GNR", 0, M), 3, A.is_lt)

    def lq(q, name="LQ"): return b(name, 128 * q, 128 * q + 128)
    for q in range(16):
        mm(b("M0", 0, 220), lq(q), b("GLR", q, M, 16), q == 0, False)
    for k in range(4):
        c = (880 * k, 880 * k + 880)
        if k == 3: ts(b("NE", *c), b("SI", *c), M, A.not_equal)
        cp(b("SN", *c), b("SI", *c))
        if k < 3: act(b("NE", *c), b("SN", *c), F.Sign, bias=3520.0, scale=-1.0)
    for q in range(16):
        mm(b("M0", 0, 220), lq(q), b("NE", q, M, 16), False, q == 15)
    ts(b("TM"), b("TMP"), -1.0, A.mult)
    ts(b("I255"), b("IDN"), -255.0, A.mult)
    tt(b("TMX"), b("TM"), b("I255"), A.add)
    fill(b("ONEF"), 1.0)
    ts(b("JK"), b("IM"), QC, A.add)
    ts(b("JS"), b("JK"), -3472.0, A.add)
    ts(b("BJ"), b("JK"), -3663.5, A.add)
    ts(b("IP"), b("IP"), 15, A.bitwise_and)
    ts(b("MASK"), b("IP"), 0, A.is_equal)
    ts(b("RES"), b("L15"), 0, A.not_equal)
    def late_constants():
        ts(b("LQQ"), b("LQ"), Q16, A.mult)
        more_fathers()
        ts(b("RESB"), b("RES"), -1e12, A.mult, 1e12, A.add)
        ts(b("IDN4"), b("IDN"), 4096.0, A.mult)
        ts(b("NEGI"), b("IDN"), -1.0, A.mult)
        ts(b("NTHI"), b("IDN"), -524288.0, A.mult)
        ts(b("BIGI"), b("IDN"), 4194304.0, A.mult)
        ts(b("QD0"), b("IDN"), H0, A.mult)
        ts(b("QD1"), b("IDN"), H1, A.mult)
        ts(b("QO0"), b("SHU"), H0, A.mult)
        ts(b("QO1"), b("SHD"), H1, A.mult)

    def later_constants():
        ts(W16, b("WT"), 0.0625, A.mult)
        ts(b("NBO"), b("BO"), -1.0, A.mult)
        for j in (0, 12): cp(b("JK2", j, j + 12), b("JK"))
        ts(QP, b("PQ", 0, 1), 1.0, A.add)
        for k in "YS":
            ts(b("EZ" + k), b("L15", 0, 192), QP, A.is_equal, -20000.0, A.mult)
        cp(b("ARO"), b("I1", 0, 64))
        ts(b("TRI2"), b("TRI"), 2.0, A.mult)
        tt(b("TRI2"), b("TRI2"), b("IDN"), A.subtract)
        ts(b("NEWT"), b("I1", 0, 64), 3536.0, A.add, E1c, A.mult)

    def weave(*parts):
        parts = [iter(p) for p in parts]
        while parts:
            parts = [p for p in parts if next(p, p) is not p]

    def lg(j, n=12, lo=0): return b("LG", 12 * j + lo, 12 * j + lo + n)

    def diag(out, x, n, g1="G1", g2="G2"):
        tt(b(g1, 0, n), x, b("MASK", 0, n), A.mult)
        scan(b(g2, 0, n), b("RES", 0, n), b(g1, 0, n), 0.0, A.mult, A.add)
        cp(out, b(g2, 15, n, 16))

    def recount():
        mm(b("M0", 0, NB), b("IDN"), b("NOK", 0, NB), True, False)
        for q in range(16):
            mm(b("M0", 0, NB), lq(q), b("ADD", q, W, 16), False, q == 15)

    def lanes(t, meanwhile):
        r = 107 * t % NB
        sign = SIGN[1 if t else 0]
        if t == 0:
            ts(b("OKR", 0, 220), b("M0", 0, 220), 0, A.is_equal)
            ts(b("NOK", 0, 220), b("M0", 0, 220), 0, A.not_equal)
        else:
            ts(b("OKR", 0, NB - r), b("M0", r, NB), 0, A.is_equal)
            ts(b("OKR", NB - r, NB), b("M0", 0, r), 0, A.is_equal)
        mm(b("M1", 0, NB), b("BO"), b("OKR", 0, NB), True, True)
        mm(b("M1", 240, 240 + NB), b("TMX"), b("OKR", 0, NB), True, True)
        scan(b("SB", 0, NB), b("ONEF", 0, NB), b("M1", 0, NB), 0.0, A.mult, A.add)
        for m in range(sign):
            act(b("SJ", 0, NB), b("SB", 0, NB), F.Sign, bias=c1("BJ", m), scale=-1.0, accum_out=c1("KA", m))
        tt(b("PL", 0, NB), b("M1", 240, 240 + NB), b("SB", 0, NB), A.add)
        for m in range(sign, 12):
            ts(b("CM%d" % (m % 2), 0, NB), b("SB", 0, NB), c1("BJ", m), A.is_le)
            call("v", V.tensor_reduce, c1("KA", m), [b("CM%d" % (m % 2), 0, NB)], [AxisListType.X, A.add], {})
        if t:
            LX = "LX%d" % t
            arrive((rank - t) % N, LX, "snd_in%d" % (t - 1))
            act(b("XLR", 0, 512), ind(LX, b("ARO", 0, 32), hi=64), F.Copy)
            act(b("XLR", 3584, 4096), ind(LX, b("ARO", 32, 64), hi=64), F.Copy)
        meanwhile()
        ts(b("KO", 0, sign), b("KA", 0, sign), 0.5, A.mult, NB / 2.0, A.add)
        if sign < 12: cp(b("KO", sign, 12), b("KA", sign, 12))
        ts(b("KA", 0, sign), b("KA", 0, sign), 0.5, A.mult, NB / 2.0, A.add)
        tt(b("OH"), ind("PL", b("KO"), hi=240), b("JREP"), A.is_equal)
        for q in range(16):
            mm(b("M0", 0, 12), lq(q, "LQQ"), b("OH", q, 192, 16), q == 0, q == 15)
        ts(b("HT"), b("KA"), NB - r, A.is_ge, -float(NB), A.mult)
        ts(b("HE"), b("KA"), NB, A.is_ge, 3520.0 - 16 * r, A.mult)
        tt(b("HT"), b("HT"), b("KA"), A.add)
        ts(b("HB"), b("HT"), 16.0, A.mult, 16.0 * r, A.add)
        tt(b("HB"), b("HB"), b("HE"), A.add)
        tt(b("H"), b("M0", 0, 12), b("HB"), A.add)
        cp(b("HU"), b("H"))

    def climb(F_, src, out):
        ts(b("PX"), src, 64, A.is_lt, float(EXT), A.mult)
        yield
        tt(b("PX"), b("PX"), src, A.add)
        yield
        cp(b("PU"), b("PX"))
        yield
        tt(b("G1"), ind(F_, b("PU")), b("MASK", 0, 192), A.mult)
        yield
        scan(b("G2"), b("RES", 0, 192), b("G1"), 0.0, A.mult, A.add)
        yield
        cp(out, b("G2", 15, 192, 16))
        yield

    def starts(t):
        F_ = "F2" if t % 2 else "F1"
        cp(b("HRU"), ind("IOTA", b("HU")))
        act(b("XLR", 1024, 2048), ind("X", b("HRU", 32, 96)), F.Copy)
        tt(b("G1"), ind(F_, b("HU")), b("MASK", 0, 192), A.mult)
        scan(b("G2"), b("RES", 0, 192), b("G1"), 0.0, A.mult, A.add)
        cp(b("CU", 2, 14), b("G2", 15, 192, 16))

    def arrivals(t):
        if t:
            if t == 1: fill(b("EQA", 0, 32), 0.0)
            LX = "LX%d" % t
            for q in range(16):
                mm(b("M1", 0, 4), lq(q, "LW"), b(LX, q, 64, 16), q == 0, q == 15)
            yield
            cp(b("HI", 0, 4), b("M1", 0, 4))
            yield
            ts(b("HI", 0, 4), b("HI", 0, 4), 63, A.bitwise_and)
            yield
            cp(b("CU", 0, 2), b("HI", 0, 2))
            cp(b("CU", 14, 16), b("HI", 2, 4))

    def starts_b(t):
        act(b("XLR", 2048, 3584), ind("X", b("HRU", 96, 192)), F.Copy)

    def sg_at(z, lo, hi): return b("KEY" + z, 256 + lo, 256 + hi)

    def hist(e, lo, hi): return b("HI", 16 * e + lo, 16 * e + hi)

    def rng(t, z):
        if z == "A": return (0 if t else 2), 8, 2, 8
        return 8, (16 if t else 14), 8, 14

    TC, REAL, DQ, DP, ALB, TA, TB, FO, YLs = range(9)
    UP = {1: "UP1", 2: "UP2"}

    def front(t, e, z, between=None, behind=None):
        k0, k1, o0, o1 = rng(t, z)
        kc = k1 - k0
        n = 16 * kc
        ks = KS[1 if t else 0][e - 1]
        kv = kc - ks
        cu = b("CU", k0, k1)
        su, df, xg, sg, dd, pw, key = "SU" + z, "DF" + z, "XG" + z, "SG" + z, "D3" + z, "PW" + z, "KEY" + z
        sub = ("SUB0", "M0") if z == "A" else ("SUB1", "M1")
        nb = kc // 2
        cp(b(su, 0, n), ind("SN", cu))
        ts(d3(sg, 0, nb), b(su, 0, n), I4 if e <= 3 else 1.0, A.add)
        if between: between()
        for P in (0, 1):
            mm(d3(pw, 0, nb, 16 * P, 16 * P + 16), b("QD%d" % P), d3(sg, 0, nb, 16 * P, 16 * P + 16), True, False)
            mm(d3(pw, 0, nb, 16 * P, 16 * P + 16), b("QO%d" % P), d3(sg, 0, nb, 16 - 16 * P, 32 - 16 * P), False, True)
        flush()
        act(b(xg, 0, 256 * ks), ind("X", b(su, 16 * kv, n)), F.Copy)
        if behind: behind()
        x0 = 256 * k0
        c4 = min(kv, 4)
        tt(b(df, 0, 256 * kv), ind("X", b(su, 0, 16 * kv)), b("XLR", x0, x0 + 256 * kv), A.subtract)
        yield
        subs = [(kv + 2 * j, min(kv + 2 * j + 2, kc), sub[j]) for j in range((ks + 1) // 2)]
        for lo, hi, bank in subs:
            w = 256 * (hi - lo)
            mm(b(bank, 0, w), b("IDN"), b(xg, 256 * (lo - kv), 256 * (hi - kv)), True, False)
            mm(b(bank, 0, w), b("NEGI"), b("XLR", x0 + 256 * lo, x0 + 256 * hi), False, True)
        act(d3(dd, 0, kv), b(df, 0, 256 * kv), F.Abs)
        for lo, hi, bank in subs:
            act(d3(dd, lo, hi), b(bank, 0, 256 * (hi - lo)), F.Abs)
        sig = sg_at(z, 0, n)
        if e <= 3:
            i0, i1 = o0 - k0, o1 - k0
            m0, m1 = o0 - 2, o1 - 2
            ex = b("EX" + z, 16 * i0, 16 * i1, 16)
            L = m1 - m0
            my, ta = "MX" + z, lg(TA, L, m0)
            if e == 1:
                ts(ex, b("H", m0, m1), 4096.0, A.add)
            else:
                Z = b("ZD%d" % (e - 1), o0, o1)
                ts(Z, b(my, 16 * i0 + 15, 16 * i1, 16), 4096, A.is_lt)
                tt(ta, Z, b("P0P", m0, m1) if e == 2 else lg(ALB, L, m0), A.mult)
                if e == 2 and z == "B":
                    tt(lg(TB), b("ZD1", 2, 14), lg(DQ), A.mult)
                ts(ex, ta, 4095.0, A.add)
                if e == 2 and z == "B":
                    tt(b("UP2", 2, 14), lg(TB), b("UP1", 2, 14), A.add)
                    tt(lg(TC), b("ZD1", 2, 14), lg(DP), A.mult)
                    tt(lg(ALB), lg(TC), b("P0P"), A.add)
            yield
            scan(b("BX" + z, 16 * i0, 16 * i1), b("RES", 0, 16 * L), b("EX" + z, 16 * i0, 16 * i1), 0.0, A.mult, A.add)
            yield
        else:
            yield
        call("v", V.transpose, sig, [d3(pw, 0, nb)], [], {})
        yield
        if e <= 3:
            tt(b("EQ" + z, 16 * i0, 16 * i1), sg_at(z, 16 * i0, 16 * i1), b("BX" + z, 16 * i0, 16 * i1), A.is_equal)
            yield
        def keys():
            for lo, hi in ((0, c4), (c4, kc)):
                o = b(key, 16 * lo, 16 * hi)
                mm(o, b("IDN" if e <= 3 else "IDN4"), b("SLOT", 16 * lo, 16 * hi), True, False)
                if e <= 3:
                    mm(o, b("NTHI"), b("ONES", 16 * lo, 16 * hi), False, False)
                for q in range(16):
                    mm(o, lq(q, "LQ" if e <= 3 else "LQ4"), d3(dd, lo, hi, 16 * q, 16 * q + 16), False, q == 15 and e > 3)
                if e <= 3:
                    mm(o, b("BIGI"), b("EQ" + z, 16 * lo, 16 * hi), False, True)
        if t and e == 1 and z == "A":
            pending.append(keys)
        else:
            keys()

    pending = []
    def flush():
        while pending: pending.pop()()

    def back(t, e, z):
        k0, k1, o0, o1 = rng(t, z)
        kc = k1 - k0
        n = 16 * kc
        key, pm, fe, mx, sx = b("KEY" + z, 0, n), b("PM" + z, 0, n), b("FE" + z, 0, n), b("MX" + z, 0, n), b("SX" + z, 0, kc)
        if e > 3:
            ww = b("WW" + z, 0, n)
            scan(pm, b("RESB", 0, n), key, 1e12, A.add, A.min)
            yield
            tt(fe, key, pm, A.subtract)
            yield
            tt(ww, sg_at(z, 0, n), fe, A.subtract)
            yield
            scan(mx, fe, ww, 0.0, A.min, A.max)
            yield
            if e < 6:
                ts(b("CU", k0, k1), b("MX" + z, 15, n, 16), -1.0, A.add)
            ts(hist(e, k0, k1), b("MX" + z, 15, n, 16), -1.0, A.add)
            return
        scan(pm, b("RES", 0, n), key, 0.0, A.mult, A.min)
        yield
        tt(fe, key, pm, A.is_equal)
        yield
        tt(fe, sg_at(z, 0, n), fe, A.mult)
        yield
        f0 = b("FE" + z, 0, n, 16)
        if e <= 2: tt(f0, f0, b(UP[e], k0, k1), A.max)
        elif e == 3: ts(f0, f0, 3520, A.max)
        if e <= 3: yield
        scan(mx, b("RES", 0, n), fe, 0.0, A.mult, A.max)
        yield
        cp(sx, b("MX" + z, 15, n, 16))
        yield
        ts(hist(e, k0, k1), sx, 4095, A.bitwise_and)
        yield
        if e < 6:
            cp(b("CU", k0, k1), hist(e, k0, k1))

    def pair(e): return b("HI", 16 * e - 16, 16 * e + 16)
    YA, SA = b("W1", 2, 14), b("W1", 18, 30)

    def partial(t):
        for k in "12": cp(b("ZD" + k, 16, 32), b("ZD" + k, 0, 16))
        w1, w2, w3, z1, z2 = b("W1"), b("W2"), b("W3"), b("ZD1"), b("ZD2")
        tt(w1, pair(4), pair(2), A.subtract)
        yield
        tt(w3, z1, z2, A.mult)
        yield
        tt(w1, w1, z1, A.mult)
        tt(w2, z2, w3, A.subtract)
        yield
        tt(w1, w1, pair(2), A.add)
        tt(w2, w2, pair(5), A.mult)
        yield
        tt(b("T32"), w1, z2, A.mult)
        yield
        tt(w1, w1, w2, A.add)
        yield
        tt(w1, w1, b("T32"), A.subtract)
        yield
        if t:
            lx = b("LX%d" % t, 64, 80)
            for e in (3, 4, 5, 6):
                ts(b("GEM", 16 * e - 48, 16 * e - 32), lx, e, A.is_equal)
            ts(b("D16"), lx, 3, A.is_lt, 3520.0, A.mult)

    def own_found():
        tt(b("W2"), b("W3"), pair(6), A.mult)
        yield
        tt(b("W1"), b("W1"), b("W2"), A.add)
        yield
        ts(lg(FO), SA, 3520, A.not_equal)

    def give_back(t):
        rs = "RS%d" % t
        t16 = b("T16")
        tt(b("T64"), b("GEM"), b("HI", 48, 112), A.mult)
        yield
        tt(b("T32"), b("T64", 0, 32), b("T64", 32, 64), A.add)
        yield
        tt(t16, b("T32", 0, 16), b("T32", 16, 32), A.add)
        yield
        tt(t16, t16, b("D16"), A.add)
        yield
        ts(b("E16"), t16, 3520, A.is_equal)
        tt(b("E16"), b("E16"), t16, A.add)
        cp(b("RU", 0, 2), b("E16", 0, 2))
        cp(b("RU", 2, 4), b("E16", 14, 16))
        ts(b(rs, 64, 66), b("T16", 0, 2), 3520, A.not_equal)
        ts(b(rs, 66, 68), b("T16", 14, 16), 3520, A.not_equal)
        cp(b(rs, 0, 64), ind("X", b("RU")))
        remote((rank - t) % N, "RL%d" % t, rs, "ret_in%d" % t, "ret_out%d" % t)

    def send(t):
        py, SE = "PY%d" % t, b("SENT", 4 * t, 4 * t + 4)
        tt(b("LO"), lg(REAL), lg(FO), A.subtract)
        mm(b("KEYA", 0, 12), b("BO"), b("LO"), True, True)
        mm(b("KEYA", 16, 28), b("TM"), b("LO"), True, True)
        yield
        scan(lg(TC), b("ONEF", 0, 12), b("KEYA", 0, 12), 0.0, A.mult, A.add)
        yield
        tt(lg(TC), b("KEYA", 16, 28), lg(TC), A.add)
        yield
        tt(lg(TC), lg(TC), b("JS"), A.subtract)
        yield
        tt(lg(TC), lg(TC), b("LO"), A.mult)
        yield
        tt(lg(TC), lg(TC), b("JS"), A.add)
        yield
        cp(b("SLU"), lg(TC))
        yield
        sr = "SR%d" % t
        w = ind(sr, b("SLU"), hi=384)
        cp(w, b("HREP"))
        yield
        tt(b("G4"), b(sr, 0, 64), b("MASK", 0, 64), A.mult)
        yield
        scan(b("G5"), b("RES", 0, 64), b("G4"), 0.0, A.mult, A.add)
        yield
        cp(b("S4U"), b("G5", 15, 64, 16))
        cp(SE, b("G5", 15, 64, 16))
        yield
        tt(b("G4"), ind("GNR", b("S4U"), hi=W), b("MASK", 0, 64), A.mult)
        yield
        cp(b(py, 0, 64), ind("X", b("S4U")))
        scan(b("G5"), b("RES", 0, 64), b("G4"), 0.0, A.mult, A.add)
        yield
        cp(b(py, 64, 66), b("G5", 15, 32, 16))
        cp(b(py, 78, 80), b("G5", 47, 64, 16))
        remote((rank + 1 + t) % N, "LX%d" % (t + 1), py, "snd_in%d" % t, "snd_out%d" % t)

    def adopt(t):
        last = t == 2
        YL, SL, go = lg(YLs), SA, b("GO2", 0, 12)
        cp(b("LU", 12, 24), SL)
        act(b("SREP"), ind("IOTA", b("LU", 12, 24)), F.Copy)
        ts(lg(TA), YA, -3520.0, A.add)
        yield
        ts(b("NSL"), SL, -1.0, A.mult)
        yield
        tt(lg(TA), lg(TA), lg(FO), A.mult)
        off = [0]
        for k in range(11): off.append(off[-1] + 176 - 16 * k)
        for lo, hi in ((0, 4), (4, 11)):
            for k in range(lo, hi):
                act(b("EBS", off[k], off[k + 1]), b("SREP", 16 * k + 16, 192), F.Sign, bias=c1("NSL", k))
            act(b("EBT", off[lo], off[hi]), b("EBS", off[lo], off[hi]), F.Abs)
        yield
        ts(YL, lg(TA), 3520.0, A.add)
        yield
        cp(b("LU", 0, 12), YL)
        yield
        ts(b("EZS", 0, 192, 16), SL, 20000.0, A.add)
        yield
        cp(b("YREP"), ind("IOTA", b("LU", 0, 12)))
        yield
        yx, sx = b("M0", 0, 192), b("M0", 192, 384)
        scan(sx, b("RES", 0, 192), b("EZS"), 0.0, A.mult, A.add)
        yield
        ts(b("EZY", 0, 192, 16), YL, 20000.0, A.add)
        yield
        tt(b("MI"), ind("X", b("LU", 12, 24)), b("XLR", 512, 3584, 16), A.add)
        yield
        scan(yx, b("RES", 0, 192), b("EZY"), 0.0, A.mult, A.add)
        yield
        for k in range(11):
            ts(b("EBY", off[k], off[k + 1]), b("YREP", 16 * k + 16, 192), c1("LG", 12 * YLs + k), A.is_equal)
            yield
        tt(b("DGY"), b("YREP"), yx, A.is_equal)
        tt(b("DGS"), b("SREP"), sx, A.is_equal)
        mm(b("M1", 0, 192), b("BO"), b("LM"), True, False)
        mm(b("M1", 0, 192), b("BO"), b("DGY"), False, False)
        for k in range(11):
            mm(b("M1", 16 * k + 16, 192), b("BO"), b("EBY", off[k], off[k + 1]), False, False)
        mm(b("M1", 0, 192), b("BO"), b("DGS"), False, False)
        for k in range(11):
            mm(b("M1", 16 * k + 16, 192), b("NBO"), b("EBT", off[k], off[k + 1]), False, k == 10)
        cp(b("SY"), ind("SN", b("LU", 0, 12)))
        ts(b("NY"), b("SY"), 3520, A.not_equal)
        for q in range(16):
            mm(b("SUB1", 0, 12), lq(q), b("NY", q, 192, 16), q == 0, q == 15)
        if not last:
            tt(b("EA"), b("SY"), b("SREP"), A.is_equal)
            mm(b("SUB0", 0, 192), b("TRI2"), b("EA"), True, True)
            act(b("KEYB", 0, 192), b("SREP"), F.Copy, bias=3520.0, scale=-1.0)
        jk = b("JK")
        tt(b("VAL", 0, 12), SL, jk, A.subtract)
        if not last: tt(b("VAL", 12, 24), b("H"), jk, A.subtract)
        tt(b("VAL", 24, 36), YL, jk, A.subtract)
        tt(b("VAL", 36, 48), SL, jk, A.subtract)
        ts(b("MJ"), b("MI"), 1, A.arith_shift_right)
        tt(b("G1"), b("M1", 0, 192), b("MASK", 0, 192), A.mult)
        scan(b("G2"), b("RES", 0, 192), b("G1"), 0.0, A.mult, A.add)
        ts(b("M24", 0, 12), b("G2", 15, 192, 16), 0, A.is_equal)
        tt(go, b("M24", 0, 12), lg(FO), A.mult)
        tt(b("GO2", 12, 24), b("M24", 0, 12), lg(FO), A.mult)
        targets(24, "GO2", 0)
        if not last:
            cp(ind("ADD", b("LU", 36, 48)), b("ONES", 0, 192))

    def targets(at, cond, v):
        tt(b("L24"), b(cond), b("VAL", v, v + 24), A.mult)
        tt(b("L24"), b("L24"), b("JK2"), A.add)
        cp(b("LU", at, at + 24), b("L24"))

    def write_men(t):
        last = t == 2
        cp(ind("X", b("LU", 24, 36)), b("MJ"))
        if last: dma("y", T.xo[:, 0:M], b("X", 0, M), "st0")
        cp(ind("F2", b("LU", 24, 36)), b("HREP"))

    def write_first(t):
        ts(b("M24", 0, 12), b("SUB1", 0, 12), 24, A.is_gt)
        for j in (0, 12): tt(b("SV2", j, j + 12), b("M24", 0, 12), b("GO2", 0, 12), A.mult)
        targets(48, "SV2", 24)
        cp(ind("F1", b("LU", 60, 72)), b("HREP"))

    def write_sons(t):
        ts(b("HV"), b("SREP"), E0, A.mult, C0, A.add)
        yield
        ts(b("FF"), b("SUB0", 0, 192), -1, A.is_equal)
        yield
        cp(ind("SN", b("LU", 36, 48)), b("HV"))
        yield
        tt(b("KEYB", 192, 384), b("FF"), b("KEYB", 0, 192), A.mult)
        yield
        tt(b("NC"), b("KEYB", 192, 384), b("SY"), A.add)
        yield
        cp(ind("SN", b("LU", 48, 60)), b("NC"))
        yield
        if t == 1:
            ts(b("CC"), ind("SN", b("RLU", 4, 8)), N1c, A.mult)
            yield
            tt(b("CC"), b("CC"), b("NEWT"), A.add)
            yield
            cp(ind("SN", b("RLU", 4, 8)), b("CC"))

    def get_back(t):
        rl = "RL%d" % t
        SE, fl = b("SENT", 4 * (t - 1), 4 * t), b(rl, 64, 68)
        arrive((rank + t) % N, rl, "ret_in%d" % t)
        if t == 1:
            ts(b("NOK", 221, 225), fl, -1.0, A.mult, 1.0, A.add)
            tt(b("RT", 4, 8), SE, b("JK", 0, 4), A.subtract)
            tt(b("RT", 4, 8), b("RT", 4, 8), fl, A.mult)
            tt(b("RT", 4, 8), b("RT", 4, 8), b("JK", 0, 4), A.add)
            cp(b("RLU", 4, 8), b("RT", 4, 8))
            cp(ind("ADD", b("RLU", 4, 8)), b("ONES", 0, 64))

    def new_men(t):
        rl, nc = "RL%d" % t, 3536 + 64 * (t - 1)
        tt(b("RT", 0, 4), b("SENT", 4 * (t - 1), 4 * t), b(rl, 64, 68), A.mult)
        yield
        cp(b("RLU", 0, 4), b("RT", 0, 4))
        yield
        cp(b("X", nc, nc + 64), b(rl, 0, 64))
        yield
        cp(b("F1", nc, nc + 64), ind("IOTA", b("RLU", 0, 4)))
        yield
        cp(b("F2", nc, nc + 64), b("F1", nc, nc + 64))

    def rest(t):
        weave(write_sons(t), new_men(t) if t else [], arrivals(t + 1))

    for t in range(3):
        lanes(t, (lambda: rest(t - 1)) if t else late_constants)
        starts(t)
        F_ = "F2" if t % 2 else "F1"
        q1, q2 = b("UP1", 2, 14), b("Q2")

        def climbs():
            yield from climb(F_, b("P0"), q1)
            ts(b("P0P"), b("P0"), 1.0, A.add)
            yield from climb(F_, q1, q2)
            tt(lg(DQ), q2, q1, A.subtract)
            tt(lg(DP), q1, b("P0"), A.subtract)
        def at_once():
            cp(b("P0"), b("G2", 15, 192, 16))
            cp(b("XLR", 512, 1024), ind("X", b("HRU", 0, 32)))
        weave(front(t, 1, "A", at_once, lambda: starts_b(t)))
        if t < 2: ts(lg(REAL), b("H"), 3520, A.not_equal)
        weave(front(t, 1, "B", None if t else later_constants), climbs())
        act(b("HREP"), ind("IOTA", b("HU")), F.Copy)
        weave(back(t, 1, "A"))
        for e in range(2, 7):
            weave(front(t, e, "A"), back(t, e - 1, "B"))
            weave(front(t, e, "B"), back(t, e, "A"))
            if t == 0 and e < 4:
                for j in (0, 1024) if e == 2 else ():
                    act(b("LQ4", j, j + 1024), b("LQ", j, j + 1024), F.Copy, scale=4096.0)
                for j in (0, 1024) if e == 3 else ():
                    act(b("LW", j, j + 1024), b("LQ", j, j + 1024), F.Copy, scale=W16)
        flush()
        weave(partial(t))
        weave(back(t, 6, "B"))
        weave(give_back(t) if t else [], own_found())
        weave(adopt(t), send(t) if t < 2 else [])
        if t < 2:
            if t: get_back(t)
            recount()
        write_men(t)
        write_first(t)
        if t == 2:
            for k in ("F1", "F2", "X"): num(b(k, M, M + 16), 16, 0)
            dma("s", T.fo[:, 0:M], (T.F1[0:128:16, 0:M], [("F1", 0, M)]), "st1")
            dma("y", T.f2o[:, 0:M], (T.F2[0:128:16, 0:M], [("F2", 0, M)]), "st2")
            get_back(t)
            weave(new_men(t))
    dma("y", T.xo[:, M:W], b("X", M, W), "st3")
    dma("s", T.fo[:, M:W], (T.F1[0:128:16, M:W], [("F1", M, W)]), "st4")
    dma("y", T.f2o[:, M:W], (T.F2[0:128:16, M:W], [("F2", M, W)]), "st5")
    for sem, val in count.items():
        if know["g"].get(sem, 0) < val:
            g.wait_ge(T.sem[sem], val)
            know["g"][sem] = val
